import numpy as np
import ml_dtypes


def mxq(x, axis, fmt="e4m3"):
    dtype, down = {"e4m3": (ml_dtypes.float8_e4m3fn, 7), "e5m2": (ml_dtypes.float8_e5m2, 14)}[fmt]
    v = np.moveaxis(np.asarray(x, np.float32).astype(ml_dtypes.bfloat16).astype(np.float64), axis, -1)
    blocks = v.reshape(v.shape[:-1] + (-1, 32))
    amax = np.abs(blocks).max(-1, keepdims=True)
    byte = np.maximum(np.where(amax > 0, np.frexp(amax)[1] - 1 + 127, 0) - down, 1)
    scale = np.exp2(byte - 127.0)
    codes = (blocks / scale).astype(np.float32).astype(dtype).astype(np.float64)
    return np.moveaxis((codes * scale).reshape(v.shape), -1, axis)


WIDE = False


def mx_kscale(k):
    if not WIDE:
        return np.ones(k)
    levels = np.array([10, -10, 5, -5, 0])
    if k % 512:
        return np.exp2(np.random.permutation(np.resize(levels, k // 32))).repeat(32)
    a = np.empty((k // 512, 16))
    for p in range(k // 512):
        a[p, :8] = np.random.permutation(np.resize(levels, 8))
        for g in range(8):
            far = levels[np.abs(levels - a[p, g]) >= 10]
            a[p, g + 8] = far[np.random.randint(len(far))]
    return np.exp2(a.ravel()).repeat(32)


def f64(x):
    return np.asarray(x).astype(np.float64)


def striped(idx):
    return np.tile(idx.reshape(-1, 16).T, (8, 1)).astype(np.uint16)


def unstriped(offs):
    return offs[:16].T.reshape(-1).astype(np.int64)


K, T, E, C, N = 128, 4096, 2, 1024, 256


def setup_inputs():
    n = np.random.standard_normal
    idx = np.random.permutation(T)[:E * C]
    s = mx_kscale(E * C)[None, :]
    xT = n((K, T)); dyT = n((N, T))
    xT[:, idx] *= s; dyT[:, idx] /= s
    return {
        "xT": xT.astype(np.float32),
        "dyT": dyT.astype(np.float32),
        "gate": np.tile(np.random.uniform(0.2, 1.0, E * C), (N, 1)).astype(np.float32),
        "offs": striped(idx),
    }


def reference(xT, dyT, gate, offs):
    idx = unstriped(offs)
    xq = mxq(f64(xT)[:, idx], 1, "e4m3")
    gq = mxq(f64(gate) * f64(dyT)[:, idx], 1, "e4m3")
    return np.stack([(xq[:, e * C:(e + 1) * C] @ gq[:, e * C:(e + 1) * C].T) for e in range(E)])

@@ -1,0 +1,152 @@
+from contextlib import ExitStack
+
+import concourse.mybir as mybir
+from concourse.masks import make_identity
+
+K, T, E, C, N = 128, 4096, 2, 1024, 256
+S = E * C
+P = 128
+PASS = 512
+PASSES = S // PASS
+FLOPS = 2 * S * K * N
+
+F32 = mybir.dt.float32
+BF16 = mybir.dt.bfloat16
+U32 = mybir.dt.uint32
+U16 = mybir.dt.uint16
+U8 = mybir.dt.uint8
+FP8X4 = mybir.dt.float8_e4m3fn_x4
+MULT = mybir.AluOpType.mult
+
+
+def tile_moe_bdw_lin_none_kernel(tc, xT, dyT, gate, offs, out):
+    nc = tc.nc
+    with ExitStack() as ctx:
+        held = ctx.enter_context(tc.tile_pool(name="held", bufs=1))
+        turn_pool = ctx.enter_context(tc.psum_pool(name="turn", bufs=4))
+        acc_pool = ctx.enter_context(tc.psum_pool(name="acc", bufs=1))
+
+        offsets = held.tile([P, S // 16], U16, name="offsets")
+        nc.sync.dma_start(offsets[:], offs)
+
+        x_all = held.tile([P, T], F32, name="x_all")
+        dy_all = [held.tile([P, T], F32, name="dy_all0"), held.tile([P, T], F32, name="dy_all1", tag="late", align_bytes=64)]
+        gates = held.tile([P, S], F32, name="gates")
+
+        gate_rows = held.tile([P, P], F32, name="gate_rows")
+        nc.gpsimd.memset(gate_rows[32:64, :], 0.0)
+        nc.gpsimd.memset(gate_rows[64:P, :], 0.0)
+        nc.scalar.dma_start(gate_rows[0:32, :], gate[0:2, :].rearrange("o (c n) -> (o c) n", n=P))
+        nc.sync.dma_start(x_all[:], xT)
+        nc.sync.dma_start(dy_all[0][:], dyT[0:P, :])
+        nc.sync.dma_start(dy_all[1][:], dyT[P : 2 * P, :])
+
+        identity = held.tile([P, P], F32, name="identity")
+        make_identity(nc, identity[:])
+        warm = held.tile([P, 1], F32, name="warm")
+        nc.scalar.copy(out=warm[:], in_=identity[:, 0:1])
+
+        bank = turn_pool.tile([P, 4, P], F32, name="bank")
+        nc.tensor.transpose(bank[:, 0, :], gate_rows[:], identity[:])
+        gate_cols = held.tile([P, 16], F32, name="gate_cols")
+        nc.scalar.copy(out=gate_cols[:], in_=bank[:, 0, 0:16])
+        for b in range(4):
+            bank = turn_pool.tile([P, 4, P], F32, name="bank")
+            for c in range(4):
+                j = 4 * b + c
+                nc.tensor.transpose(bank[:, c, :], gate_cols[:, j : j + 1].to_broadcast([P, P]), identity[:])
+            nc.scalar.copy(out=gates[:, b * 512 : (b + 1) * 512], in_=bank[:].rearrange("p c n -> p (c n)"))
+
+        picked = [held.tile([P, S], F32, name=f"picked{s}") for s in range(3)]
+        rows = [held.tile([P, PASSES, P, 4], BF16, align_bytes=64, name=f"rows{s}") for s in range(3)]
+        codes = []
+        half = held.tile([P, PASS], BF16, name="half", align_bytes=64)
+        scales = [held.tile([P, S // 4], U8, align_bytes=64, name=f"scales{s}") for s in range(3)]
+
+        def gather(s, a, b):
+            lst = offsets[:, a // 16 : b // 16]
+            if s == 0:
+                nc.vector.tensor_copy(picked[s][:, a:b], x_all[:].indirect(lst))
+            else:
+                nc.vector.tensor_tensor(picked[s][:, a:b], dy_all[s - 1][:].indirect(lst), gates[:, a:b], MULT)
+
+        def turn(s, q):
+            bank = turn_pool.tile([P, 4, P], F32, name="bank")
+            for t in range(4):
+                nc.tensor.transpose(bank[:, t, :], picked[s][:, q * PASS + t : (q + 1) * PASS : 4], identity[:])
+            nc.scalar.copy(out=rows[s][:, q, :, :], in_=bank[:].rearrange("p t n -> p n t"))
+
+        def turn_words(src, half, q0, q1, cast):
+            cast(out=half[:], in_=src)
+            words = half[:].bitcast(F32)
+            bank = turn_pool.tile([P, q1 - q0, 2, P], F32, name="bank")
+            for q in range(q1 - q0):
+                for u in range(2):
+                    nc.tensor.transpose(bank[:, q, u, :], words[:, q * 256 + u : (q + 1) * 256 : 2], identity[:])
+            nc.scalar.copy(
+                out=rows[2][:, q0:q1, :, :].rearrange("p q n t -> p (q n t)").bitcast(F32).rearrange("p (q n u) -> p q n u", q=q1 - q0, u=2),
+                in_=bank[:].rearrange("p q u n -> p q n u"),
+            )
+
+        def quantize(s, q0, q1):
+            cols = slice(q0 * P, q1 * P)
+            nc.vector.quantize_mx(
+                out=codes[s][:, q0:q1, :].rearrange("p q n -> p (q n)").bitcast(FP8X4),
+                scales=scales[s][:, cols],
+                in_=rows[s][:, q0:q1, :, :].rearrange("p q n t -> p (q n t)"),
+            )
+
+        accs = {}
+
+        def multiply(h, q):
+            e = q // 2
+            if q % 2 == 0:
+                accs[h, e] = acc_pool.tile([P, P], F32, name=f"acc{h}{e}")
+            acc = accs[h, e]
+            cols = slice(q * P, (q + 1) * P)
+            nc.tensor.matmul_mx(
+                out=acc[:],
+                lhsT=codes[0][:, q, :].bitcast(FP8X4),
+                lhsT_scale=scales[0][:, cols],
+                rhs=codes[h + 1][:, q, :].bitcast(FP8X4),
+                rhs_scale=scales[h + 1][:, cols],
+                start=(q % 2 == 0),
+                stop=(q % 2 == 1),
+            )
+            if q % 2 == 1:
+                res = held.tile([P, P], F32, name=f"res{h}{e}")
+                nc.scalar.copy(out=res[:], in_=acc[:])
+                nc.sync.dma_start(out[e, :, h * P : (h + 1) * P], res[:])
+
+        gather(0, 0, 1024)
+        turn(0, 0)
+        turn(0, 1)
+        gather(0, 1024, 2048)
+        turn(0, 2)
+        turn(0, 3)
+        gather(1, 0, 1024)
+        turn(1, 0)
+        turn(1, 1)
+        gather(1, 1024, 2048)
+        turn(1, 2)
+        turn(1, 3)
+        gather(2, 0, 1024)
+        turn(2, 0)
+        turn(2, 1)
+        gather(2, 1024, 1536)
+        turn(2, 2)
+        gather(2, 1536, 2048)
+        turn_words(picked[2][:, 1536:2048], half, 3, 4, nc.scalar.copy)
+        late = held.tile([P, 3, 4, P], U32, name="late", tag="late", align_bytes=64)
+        codes.extend([late[:, s, :, :] for s in range(3)])
+        quantize(0, 0, 4)
+        quantize(1, 0, 4)
+        quantize(2, 0, 2)
+        quantize(2, 2, 3)
+        for q in range(4):
+            multiply(0, q)
+        multiply(1, 0)
+        multiply(1, 1)
+        multiply(1, 2)
+        quantize(2, 3, 4)
+        multiply(1, 3)

@@ -17,136 +17,135 @@ U16 = mybir.dt.uint16
 U8 = mybir.dt.uint8
 FP8X4 = mybir.dt.float8_e4m3fn_x4
 MULT = mybir.AluOpType.mult
+COPY = mybir.ActivationFunctionType.Copy
+
+CHUNKS = ((0, 1024), (1024, 2048), (2048, 3072), (3072, 4096))
+LAST = 384
+SHARE = 896
 
 
 def tile_moe_bdw_lin_none_kernel(tc, xT, dyT, gate, offs, out):
     nc = tc.nc
     with ExitStack() as ctx:
         held = ctx.enter_context(tc.tile_pool(name="held", bufs=1))
-        turn_pool = ctx.enter_context(tc.psum_pool(name="turn", bufs=4))
-        acc_pool = ctx.enter_context(tc.psum_pool(name="acc", bufs=1))
+        first = ctx.enter_context(tc.tile_pool(name="first", bufs=1))
+        psum = ctx.enter_context(tc.psum_pool(name="psum", bufs=1))
+
+        def bank(b, shape):
+            return psum.tile(shape, F32, name=f"bank{b}", tag=f"bank{b}")
 
         offsets = held.tile([P, S // 16], U16, name="offsets")
+        gate_runs = held.tile([P, 2, 8], F32, name="gate_runs")
+        x_parts = [held.tile([P, b - a], F32, name=f"x_part{a}") for a, b in CHUNKS]
+        dy_all = [first.tile([P, T], F32, name="dy_all0", offset=0, align_bytes=64), held.tile([P, T], F32, name="dy_all1", tag="dy_all1", align_bytes=64)]
+        nc.scalar.dma_start(gate_runs[:], gate[0:1, :].rearrange("o (h k j) -> k (o h) j", h=2, j=8))
         nc.sync.dma_start(offsets[:], offs)
-
-        x_all = held.tile([P, T], F32, name="x_all")
-        dy_all = [held.tile([P, T], F32, name="dy_all0"), held.tile([P, T], F32, name="dy_all1", tag="late", align_bytes=64)]
-        gates = held.tile([P, S], F32, name="gates")
-
-        gate_rows = held.tile([P, P], F32, name="gate_rows")
-        nc.gpsimd.memset(gate_rows[32:64, :], 0.0)
-        nc.gpsimd.memset(gate_rows[64:P, :], 0.0)
-        nc.scalar.dma_start(gate_rows[0:32, :], gate[0:2, :].rearrange("o (c n) -> (o c) n", n=P))
-        nc.sync.dma_start(x_all[:], xT)
         nc.sync.dma_start(dy_all[0][:], dyT[0:P, :])
+        for part, (a, b) in zip(x_parts, CHUNKS):
+            nc.sync.dma_start(part[:], xT[:, a:b])
         nc.sync.dma_start(dy_all[1][:], dyT[P : 2 * P, :])
 
         identity = held.tile([P, P], F32, name="identity")
         make_identity(nc, identity[:])
-        warm = held.tile([P, 1], F32, name="warm")
-        nc.scalar.copy(out=warm[:], in_=identity[:, 0:1])
 
-        bank = turn_pool.tile([P, 4, P], F32, name="bank")
-        nc.tensor.transpose(bank[:, 0, :], gate_rows[:], identity[:])
-        gate_cols = held.tile([P, 16], F32, name="gate_cols")
-        nc.scalar.copy(out=gate_cols[:], in_=bank[:, 0, 0:16])
-        for b in range(4):
-            bank = turn_pool.tile([P, 4, P], F32, name="bank")
-            for c in range(4):
-                j = 4 * b + c
-                nc.tensor.transpose(bank[:, c, :], gate_cols[:, j : j + 1].to_broadcast([P, P]), identity[:])
-            nc.scalar.copy(out=gates[:, b * 512 : (b + 1) * 512], in_=bank[:].rearrange("p c n -> p (c n)"))
+        gates = [held.tile([P, P, 8], F32, name=f"gates{h}") for h in range(2)]
+        for h in range(2):
+            for b in range(2):
+                spread = bank(2 * h + b, [P, 4, P])
+                for j in range(4):
+                    nc.tensor.transpose(spread[:, j, :], gate_runs[:, h, 4 * b + j : 4 * b + j + 1].to_broadcast([P, P]), identity[:])
+                nc.vector.tensor_copy(gates[h][:, :, 4 * b : 4 * b + 4], spread[:].rearrange("p j k -> p k j"))
 
-        picked = [held.tile([P, S], F32, name=f"picked{s}") for s in range(3)]
-        rows = [held.tile([P, PASSES, P, 4], BF16, align_bytes=64, name=f"rows{s}") for s in range(3)]
-        codes = []
-        half = held.tile([P, PASS], BF16, name="half", align_bytes=64)
-        scales = [held.tile([P, S // 4], U8, align_bytes=64, name=f"scales{s}") for s in range(3)]
+        x_bf = held.tile([P, T], BF16, name="x_bf")
+        rows_x = [held.tile([P, 2, P, 4], BF16, align_bytes=64, name=f"rows_x{e}") for e in range(E)]
+        scales_x = held.tile([P, S // 4], U8, align_bytes=64, name="scales_x")
+        picked_g = [held.tile([P, S], F32, name="picked_g0", tag="picked_g0", align_bytes=64)]
+        rows_g = [held.tile([P, PASSES, P, 4], BF16, align_bytes=64, name=f"rows_g{h}", tag=f"rows_g{h}") for h in range(2)]
+        scales_g = [held.tile([P, S // 4], U8, align_bytes=64, name=f"scales_g{h}") for h in range(2)]
+        last_bf = held.tile([P, PASS], BF16, name="last_bf")
+        last_rows = held.tile([P, 1, P, 4], BF16, name="last_rows", align_bytes=64)
 
-        def gather(s, a, b):
-            lst = offsets[:, a // 16 : b // 16]
-            if s == 0:
-                nc.vector.tensor_copy(picked[s][:, a:b], x_all[:].indirect(lst))
-            else:
-                nc.vector.tensor_tensor(picked[s][:, a:b], dy_all[s - 1][:].indirect(lst), gates[:, a:b], MULT)
-
-        def turn(s, q):
-            bank = turn_pool.tile([P, 4, P], F32, name="bank")
-            for t in range(4):
-                nc.tensor.transpose(bank[:, t, :], picked[s][:, q * PASS + t : (q + 1) * PASS : 4], identity[:])
-            nc.scalar.copy(out=rows[s][:, q, :, :], in_=bank[:].rearrange("p t n -> p n t"))
-
-        def turn_words(src, half, q0, q1, cast):
-            cast(out=half[:], in_=src)
-            words = half[:].bitcast(F32)
-            bank = turn_pool.tile([P, q1 - q0, 2, P], F32, name="bank")
-            for q in range(q1 - q0):
+        def turn_words(srcs, rows, b):
+            passes = len(srcs)
+            turned = bank(b, [P, passes, 2, P])
+            for q in range(passes):
                 for u in range(2):
-                    nc.tensor.transpose(bank[:, q, u, :], words[:, q * 256 + u : (q + 1) * 256 : 2], identity[:])
+                    nc.tensor.transpose(turned[:, q, u, :], srcs[q].bitcast(F32)[:, u:256:2], identity[:])
             nc.scalar.copy(
-                out=rows[2][:, q0:q1, :, :].rearrange("p q n t -> p (q n t)").bitcast(F32).rearrange("p (q n u) -> p q n u", q=q1 - q0, u=2),
-                in_=bank[:].rearrange("p q u n -> p q n u"),
+                out=rows.rearrange("p q n t -> p (q n t)").bitcast(F32).rearrange("p (q n u) -> p q n u", q=passes, u=2),
+                in_=turned[:].rearrange("p q u n -> p q n u"),
             )
 
-        def quantize(s, q0, q1):
-            cols = slice(q0 * P, q1 * P)
+        def quantize(codes, scales, rows):
             nc.vector.quantize_mx(
-                out=codes[s][:, q0:q1, :].rearrange("p q n -> p (q n)").bitcast(FP8X4),
-                scales=scales[s][:, cols],
-                in_=rows[s][:, q0:q1, :, :].rearrange("p q n t -> p (q n t)"),
+                out=codes.rearrange("p q n -> p (q n)").bitcast(FP8X4),
+                scales=scales,
+                in_=rows.rearrange("p q n t -> p (q n t)"),
             )
 
-        accs = {}
+        def gather_g(h, a, b):
+            gate_cols = gates[a // C][:].rearrange("p k j -> p (k j)")[:, a % C : a % C + b - a]
+            nc.vector.tensor_tensor(picked_g[h][:, a:b], dy_all[h][:].indirect(offsets[:, a // 16 : b // 16]), gate_cols, MULT)
 
-        def multiply(h, q):
+        def turn_g(h, q, b, copy):
+            turned = bank(b, [P, 4, P])
+            for t in range(4):
+                nc.tensor.transpose(turned[:, t, :], picked_g[h][:, q * PASS + t : (q + 1) * PASS : 4], identity[:])
+            copy(out=rows_g[h][:, q, :, :], in_=turned[:].rearrange("p t n -> p n t"))
+
+        for q in range(PASSES):
+            gather_g(0, q * PASS, (q + 1) * PASS)
+        for part, (a, b) in zip(x_parts, CHUNKS):
+            nc.scalar.copy(out=x_bf[:, a:b], in_=part[:])
+        for q in range(PASSES):
+            turn_g(0, q, 4 + q, nc.vector.tensor_copy if q == 0 else nc.scalar.copy)
+
+        early_x = first.tile([P, PASS], BF16, name="early_x", offset=0, align_bytes=64)
+        later_x = held.tile([P, S - PASS], BF16, name="later_x", tag="picked_g0", align_bytes=64)
+        nc.vector.tensor_copy(early_x[:], x_bf[:].indirect(offsets[:, 0 : PASS // 16]))
+        nc.vector.tensor_copy(later_x[:, 0 : SHARE - PASS], x_bf[:].indirect(offsets[:, PASS // 16 : SHARE // 16]))
+        nc.scalar.activation(later_x[:, SHARE - PASS :], x_bf[:].indirect(offsets[:, SHARE // 16 : S // 16]), COPY)
+        turn_words([early_x[:], later_x[:, 0:PASS]], rows_x[0][:], 0)
+        turn_words([later_x[:, PASS : 2 * PASS], later_x[:, 2 * PASS :]], rows_x[1][:], 1)
+        codes_g0 = first.tile([P, PASSES, P], U32, name="codes_g0", offset=0, align_bytes=64)
+        quantize(codes_g0[:], scales_g[0][:], rows_g[0][:])
+
+        picked_g.append(held.tile([P, S], F32, name="picked_g1", tag="rows_g0", align_bytes=64))
+        for q in range(3):
+            gather_g(1, q * PASS, (q + 1) * PASS)
+            turn_g(1, q, 3 + q, nc.scalar.copy)
+        gather_g(1, 1536, 1536 + LAST)
+        gather_g(1, 1536 + LAST, S)
+        nc.vector.tensor_copy(last_bf[:, 0:LAST], picked_g[1][:, 1536 : 1536 + LAST])
+        nc.vector.tensor_copy(last_bf[:, LAST:PASS], picked_g[1][:, 1536 + LAST : S])
+        turn_words([last_bf[:]], last_rows[:], 6)
+
+        late = held.tile([P, 2, PASSES, P], U32, name="late", tag="dy_all1", align_bytes=64)
+        codes_x = late[:, 0, :, :]
+        codes_g = [codes_g0[:], late[:, 1, :, :]]
+        quantize(codes_x[:, 2:4, :], scales_x[:, 2 * P : 4 * P], rows_x[1][:])
+        quantize(codes_g[1][:, 2:3, :], scales_g[1][:, 2 * P : 3 * P], rows_g[1][:, 2:3, :, :])
+        quantize(codes_x[:, 0:2, :], scales_x[:, 0 : 2 * P], rows_x[0][:])
+        quantize(codes_g[1][:, 0:2, :], scales_g[1][:, 0 : 2 * P], rows_g[1][:, 0:2, :, :])
+        quantize(codes_g[1][:, 3:4, :], scales_g[1][:, 3 * P : 4 * P], last_rows[:])
+
+        accs = {(0, 1): bank(7, [P, P]), (1, 1): bank(0, [P, P]), (0, 0): bank(1, [P, P]), (1, 0): bank(2, [P, P])}
+        for h, q in ((0, 2), (0, 3), (1, 2), (0, 0), (0, 1), (1, 0), (1, 1), (1, 3)):
             e = q // 2
-            if q % 2 == 0:
-                accs[h, e] = acc_pool.tile([P, P], F32, name=f"acc{h}{e}")
-            acc = accs[h, e]
             cols = slice(q * P, (q + 1) * P)
             nc.tensor.matmul_mx(
-                out=acc[:],
-                lhsT=codes[0][:, q, :].bitcast(FP8X4),
-                lhsT_scale=scales[0][:, cols],
-                rhs=codes[h + 1][:, q, :].bitcast(FP8X4),
-                rhs_scale=scales[h + 1][:, cols],
+                out=accs[h, e][:],
+                lhsT=codes_x[:, q, :].bitcast(FP8X4),
+                lhsT_scale=scales_x[:, cols],
+                rhs=codes_g[h][:, q, :].bitcast(FP8X4),
+                rhs_scale=scales_g[h][:, cols],
                 start=(q % 2 == 0),
                 stop=(q % 2 == 1),
             )
             if q % 2 == 1:
                 res = held.tile([P, P], F32, name=f"res{h}{e}")
-                nc.scalar.copy(out=res[:], in_=acc[:])
+                if (h, q) == (1, 3):
+                    nc.vector.tensor_copy(res[:], accs[h, e][:])
+                else:
+                    nc.scalar.copy(out=res[:], in_=accs[h, e][:])
                 nc.sync.dma_start(out[e, :, h * P : (h + 1) * P], res[:])
-
-        gather(0, 0, 1024)
-        turn(0, 0)
-        turn(0, 1)
-        gather(0, 1024, 2048)
-        turn(0, 2)
-        turn(0, 3)
-        gather(1, 0, 1024)
-        turn(1, 0)
-        turn(1, 1)
-        gather(1, 1024, 2048)
-        turn(1, 2)
-        turn(1, 3)
-        gather(2, 0, 1024)
-        turn(2, 0)
-        turn(2, 1)
-        gather(2, 1024, 1536)
-        turn(2, 2)
-        gather(2, 1536, 2048)
-        turn_words(picked[2][:, 1536:2048], half, 3, 4, nc.scalar.copy)
-        late = held.tile([P, 3, 4, P], U32, name="late", tag="late", align_bytes=64)
-        codes.extend([late[:, s, :, :] for s in range(3)])
-        quantize(0, 0, 4)
-        quantize(1, 0, 4)
-        quantize(2, 0, 2)
-        quantize(2, 2, 3)
-        for q in range(4):
-            multiply(0, q)
-        multiply(1, 0)
-        multiply(1, 1)
-        multiply(1, 2)
-        quantize(2, 3, 4)
-        multiply(1, 3)

@@ -19,9 +19,9 @@ FP8X4 = mybir.dt.float8_e4m3fn_x4
 MULT = mybir.AluOpType.mult
 COPY = mybir.ActivationFunctionType.Copy
 
-CHUNKS = ((0, 1024), (1024, 2048), (2048, 3072), (3072, 4096))
+CHUNKS = ((0, 1536), (1536, 3072), (3072, 4096))
 LAST = 384
-SHARE = 896
+SHARE = 640
 
 
 def tile_moe_bdw_lin_none_kernel(tc, xT, dyT, gate, offs, out):
@@ -35,10 +35,10 @@ def tile_moe_bdw_lin_none_kernel(tc, xT, dyT, gate, offs, out):
             return psum.tile(shape, F32, name=f"bank{b}", tag=f"bank{b}")
 
         offsets = held.tile([P, S // 16], U16, name="offsets")
-        gate_runs = held.tile([P, 2, 8], F32, name="gate_runs")
-        x_parts = [held.tile([P, b - a], F32, name=f"x_part{a}") for a, b in CHUNKS]
-        dy_all = [first.tile([P, T], F32, name="dy_all0", offset=0, align_bytes=64), held.tile([P, T], F32, name="dy_all1", tag="dy_all1", align_bytes=64)]
-        nc.scalar.dma_start(gate_runs[:], gate[0:1, :].rearrange("o (h k j) -> k (o h) j", h=2, j=8))
+        gate_runs = held.tile([P, 16], F32, name="gate_runs")
+        x_parts = [held.tile([P, b - a], F32, name=f"x_part{a}", tag=f"x_part{a}", align_bytes=64) for a, b in CHUNKS]
+        dy_all = [held.tile([P, T], F32, name="dy_all0"), held.tile([P, T], F32, name="dy_all1", tag="dy_all1", align_bytes=64)]
+        nc.scalar.dma_start(gate_runs[:], gate[0:1, :].rearrange("o (k j) -> k (o j)", j=16))
         nc.sync.dma_start(offsets[:], offs)
         nc.sync.dma_start(dy_all[0][:], dyT[0:P, :])
         for part, (a, b) in zip(x_parts, CHUNKS):
@@ -48,19 +48,18 @@ def tile_moe_bdw_lin_none_kernel(tc, xT, dyT, gate, offs, out):
         identity = held.tile([P, P], F32, name="identity")
         make_identity(nc, identity[:])
 
-        gates = [held.tile([P, P, 8], F32, name=f"gates{h}") for h in range(2)]
-        for h in range(2):
-            for b in range(2):
-                spread = bank(2 * h + b, [P, 4, P])
-                for j in range(4):
-                    nc.tensor.transpose(spread[:, j, :], gate_runs[:, h, 4 * b + j : 4 * b + j + 1].to_broadcast([P, P]), identity[:])
-                nc.vector.tensor_copy(gates[h][:, :, 4 * b : 4 * b + 4], spread[:].rearrange("p j k -> p k j"))
+        gates = held.tile([P, P, 16], F32, name="gates")
+        for b in range(4):
+            spread = bank(b, [P, 4, P])
+            for j in range(4):
+                nc.tensor.transpose(spread[:, j, :], gate_runs[:, 4 * b + j : 4 * b + j + 1].to_broadcast([P, P]), identity[:])
+            nc.vector.tensor_copy(gates[:, :, 4 * b : 4 * b + 4], spread[:].rearrange("p j k -> p k j"))
 
         x_bf = held.tile([P, T], BF16, name="x_bf")
         rows_x = [held.tile([P, 2, P, 4], BF16, align_bytes=64, name=f"rows_x{e}") for e in range(E)]
         scales_x = held.tile([P, S // 4], U8, align_bytes=64, name="scales_x")
-        picked_g = [held.tile([P, S], F32, name="picked_g0", tag="picked_g0", align_bytes=64)]
-        rows_g = [held.tile([P, PASSES, P, 4], BF16, align_bytes=64, name=f"rows_g{h}", tag=f"rows_g{h}") for h in range(2)]
+        picked_g = [first.tile([P, S], F32, name="picked_g0", offset=0, align_bytes=64)]
+        rows_g1 = held.tile([P, PASSES, P, 4], BF16, align_bytes=64, name="rows_g1")
         scales_g = [held.tile([P, S // 4], U8, align_bytes=64, name=f"scales_g{h}") for h in range(2)]
         last_bf = held.tile([P, PASS], BF16, name="last_bf")
         last_rows = held.tile([P, 1, P, 4], BF16, name="last_rows", align_bytes=64)
@@ -84,36 +83,41 @@ def tile_moe_bdw_lin_none_kernel(tc, xT, dyT, gate, offs, out):
             )
 
         def gather_g(h, a, b):
-            gate_cols = gates[a // C][:].rearrange("p k j -> p (k j)")[:, a % C : a % C + b - a]
+            gate_cols = gates[:].rearrange("p k j -> p (k j)")[:, a:b]
             nc.vector.tensor_tensor(picked_g[h][:, a:b], dy_all[h][:].indirect(offsets[:, a // 16 : b // 16]), gate_cols, MULT)
 
-        def turn_g(h, q, b, copy):
+        def turn_g(h, q, b, rows, copy):
             turned = bank(b, [P, 4, P])
             for t in range(4):
                 nc.tensor.transpose(turned[:, t, :], picked_g[h][:, q * PASS + t : (q + 1) * PASS : 4], identity[:])
-            copy(out=rows_g[h][:, q, :, :], in_=turned[:].rearrange("p t n -> p n t"))
+            copy(out=rows, in_=turned[:].rearrange("p t n -> p n t"))
 
         for q in range(PASSES):
             gather_g(0, q * PASS, (q + 1) * PASS)
         for part, (a, b) in zip(x_parts, CHUNKS):
             nc.scalar.copy(out=x_bf[:, a:b], in_=part[:])
+        rows_g0 = [
+            held.tile([P, 2, P, 4], BF16, align_bytes=64, name="rows_g0a"),
+            held.tile([P, 2, P, 4], BF16, align_bytes=64, name="rows_g0b", tag=f"x_part{CHUNKS[-1][0]}"),
+        ]
         for q in range(PASSES):
-            turn_g(0, q, 4 + q, nc.vector.tensor_copy if q == 0 else nc.scalar.copy)
+            turn_g(0, q, 4 + q, rows_g0[q // 2][:, q % 2, :, :], nc.vector.tensor_copy if q < 2 else nc.scalar.copy)
 
         early_x = first.tile([P, PASS], BF16, name="early_x", offset=0, align_bytes=64)
-        later_x = held.tile([P, S - PASS], BF16, name="later_x", tag="picked_g0", align_bytes=64)
+        later_x = first.tile([P, S - PASS], BF16, name="later_x", offset=4096, align_bytes=64)
         nc.vector.tensor_copy(early_x[:], x_bf[:].indirect(offsets[:, 0 : PASS // 16]))
         nc.vector.tensor_copy(later_x[:, 0 : SHARE - PASS], x_bf[:].indirect(offsets[:, PASS // 16 : SHARE // 16]))
         nc.scalar.activation(later_x[:, SHARE - PASS :], x_bf[:].indirect(offsets[:, SHARE // 16 : S // 16]), COPY)
         turn_words([early_x[:], later_x[:, 0:PASS]], rows_x[0][:], 0)
         turn_words([later_x[:, PASS : 2 * PASS], later_x[:, 2 * PASS :]], rows_x[1][:], 1)
-        codes_g0 = first.tile([P, PASSES, P], U32, name="codes_g0", offset=0, align_bytes=64)
-        quantize(codes_g0[:], scales_g[0][:], rows_g[0][:])
+        codes_g0 = held.tile([P, PASSES, P], U32, name="codes_g0", align_bytes=64)
+        for e in range(E):
+            quantize(codes_g0[:, 2 * e : 2 * e + 2, :], scales_g[0][:, 2 * e * P : (2 * e + 2) * P], rows_g0[e][:])
 
-        picked_g.append(held.tile([P, S], F32, name="picked_g1", tag="rows_g0", align_bytes=64))
+        picked_g.append(held.tile([P, S], F32, name="picked_g1", tag=f"x_part{CHUNKS[-1][0]}", align_bytes=64))
         for q in range(3):
             gather_g(1, q * PASS, (q + 1) * PASS)
-            turn_g(1, q, 3 + q, nc.scalar.copy)
+            turn_g(1, q, 3 + q, rows_g1[:, q, :, :], nc.scalar.copy)
         gather_g(1, 1536, 1536 + LAST)
         gather_g(1, 1536 + LAST, S)
         nc.vector.tensor_copy(last_bf[:, 0:LAST], picked_g[1][:, 1536 : 1536 + LAST])
@@ -124,9 +128,9 @@ def tile_moe_bdw_lin_none_kernel(tc, xT, dyT, gate, offs, out):
         codes_x = late[:, 0, :, :]
         codes_g = [codes_g0[:], late[:, 1, :, :]]
         quantize(codes_x[:, 2:4, :], scales_x[:, 2 * P : 4 * P], rows_x[1][:])
-        quantize(codes_g[1][:, 2:3, :], scales_g[1][:, 2 * P : 3 * P], rows_g[1][:, 2:3, :, :])
+        quantize(codes_g[1][:, 2:3, :], scales_g[1][:, 2 * P : 3 * P], rows_g1[:, 2:3, :, :])
         quantize(codes_x[:, 0:2, :], scales_x[:, 0 : 2 * P], rows_x[0][:])
-        quantize(codes_g[1][:, 0:2, :], scales_g[1][:, 0 : 2 * P], rows_g[1][:, 0:2, :, :])
+        quantize(codes_g[1][:, 0:2, :], scales_g[1][:, 0 : 2 * P], rows_g1[:, 0:2, :, :])
         quantize(codes_g[1][:, 3:4, :], scales_g[1][:, 3 * P : 4 * P], last_rows[:])
 
         accs = {(0, 1): bank(7, [P, P]), (1, 1): bank(0, [P, P]), (0, 0): bank(1, [P, P]), (1, 0): bank(2, [P, P])}

@@ -21,7 +21,7 @@ COPY = mybir.ActivationFunctionType.Copy
 
 CHUNKS = ((0, 1536), (1536, 3072), (3072, 4096))
 LAST = 384
-SHARE = 640
+SHARE = 512
 
 
 def tile_moe_bdw_lin_none_kernel(tc, xT, dyT, gate, offs, out):
@@ -106,7 +106,6 @@ def tile_moe_bdw_lin_none_kernel(tc, xT, dyT, gate, offs, out):
         early_x = first.tile([P, PASS], BF16, name="early_x", offset=0, align_bytes=64)
         later_x = first.tile([P, S - PASS], BF16, name="later_x", offset=4096, align_bytes=64)
         nc.vector.tensor_copy(early_x[:], x_bf[:].indirect(offsets[:, 0 : PASS // 16]))
-        nc.vector.tensor_copy(later_x[:, 0 : SHARE - PASS], x_bf[:].indirect(offsets[:, PASS // 16 : SHARE // 16]))
         nc.scalar.activation(later_x[:, SHARE - PASS :], x_bf[:].indirect(offsets[:, SHARE // 16 : S // 16]), COPY)
         turn_words([early_x[:], later_x[:, 0:PASS]], rows_x[0][:], 0)
         turn_words([later_x[:, PASS : 2 * PASS], later_x[:, 2 * PASS :]], rows_x[1][:], 1)

@@ -127,13 +127,13 @@ def tile_moe_bdw_lin_none_kernel(tc, xT, dyT, gate, offs, out):
         codes_x = late[:, 0, :, :]
         codes_g = [codes_g0[:], late[:, 1, :, :]]
         quantize(codes_x[:, 2:4, :], scales_x[:, 2 * P : 4 * P], rows_x[1][:])
-        quantize(codes_g[1][:, 2:3, :], scales_g[1][:, 2 * P : 3 * P], rows_g1[:, 2:3, :, :])
         quantize(codes_x[:, 0:2, :], scales_x[:, 0 : 2 * P], rows_x[0][:])
         quantize(codes_g[1][:, 0:2, :], scales_g[1][:, 0 : 2 * P], rows_g1[:, 0:2, :, :])
+        quantize(codes_g[1][:, 2:3, :], scales_g[1][:, 2 * P : 3 * P], rows_g1[:, 2:3, :, :])
         quantize(codes_g[1][:, 3:4, :], scales_g[1][:, 3 * P : 4 * P], last_rows[:])
 
         accs = {(0, 1): bank(7, [P, P]), (1, 1): bank(0, [P, P]), (0, 0): bank(1, [P, P]), (1, 0): bank(2, [P, P])}
-        for h, q in ((0, 2), (0, 3), (1, 2), (0, 0), (0, 1), (1, 0), (1, 1), (1, 3)):
+        for h, q in ((0, 2), (0, 3), (0, 0), (0, 1), (1, 0), (1, 1), (1, 2), (1, 3)):
             e = q // 2
             cols = slice(q * P, (q + 1) * P)
             nc.tensor.matmul_mx(

@@ -38,12 +38,12 @@ def tile_moe_bdw_lin_none_kernel(tc, xT, dyT, gate, offs, out):
         gate_runs = held.tile([P, 16], F32, name="gate_runs")
         x_parts = [held.tile([P, b - a], F32, name=f"x_part{a}", tag=f"x_part{a}", align_bytes=64) for a, b in CHUNKS]
         dy_all = [held.tile([P, T], F32, name="dy_all0"), held.tile([P, T], F32, name="dy_all1", tag="dy_all1", align_bytes=64)]
-        nc.scalar.dma_start(gate_runs[:], gate[0:1, :].rearrange("o (k j) -> k (o j)", j=16))
+        nc.sync.dma_start(gate_runs[:], gate[0:1, :].rearrange("o (k j) -> k (o j)", j=16))
         nc.sync.dma_start(offsets[:], offs)
-        nc.sync.dma_start(dy_all[0][:], dyT[0:P, :])
+        nc.scalar.dma_start(dy_all[0][:], dyT[0:P, :])
         for part, (a, b) in zip(x_parts, CHUNKS):
-            nc.sync.dma_start(part[:], xT[:, a:b])
-        nc.sync.dma_start(dy_all[1][:], dyT[P : 2 * P, :])
+            nc.scalar.dma_start(part[:], xT[:, a:b])
+        nc.scalar.dma_start(dy_all[1][:], dyT[P : 2 * P, :])
 
         identity = held.tile([P, P], F32, name="identity")
         make_identity(nc, identity[:])

@@ -119,9 +119,19 @@ def tile_moe_bdw_lin_none_kernel(tc, xT, dyT, gate, offs, out):
             turn_g(1, q, 3 + q, rows_g1[:, q, :, :], nc.scalar.copy)
         gather_g(1, 1536, 1536 + LAST)
         gather_g(1, 1536 + LAST, S)
-        nc.vector.tensor_copy(last_bf[:, 0:LAST], picked_g[1][:, 1536 : 1536 + LAST])
-        nc.vector.tensor_copy(last_bf[:, LAST:PASS], picked_g[1][:, 1536 + LAST : S])
-        turn_words([last_bf[:]], last_rows[:], 6)
+        last_halves = last_bf[:].rearrange("p (u w e) -> p u w e", u=2, e=2)
+        for a, b in ((0, LAST), (LAST, PASS)):
+            nc.vector.tensor_copy(
+                last_halves[:, :, a // 4 : b // 4, :],
+                picked_g[1][:, 1536 + a : 1536 + b].rearrange("p (w u e) -> p u w e", u=2, e=2),
+            )
+        turned = bank(6, [P, 2, P])
+        for u in range(2):
+            nc.tensor.transpose(turned[:, u, :], last_bf[:].bitcast(F32)[:, u * P : (u + 1) * P], identity[:])
+        nc.scalar.copy(
+            out=last_rows[:].rearrange("p q n t -> p (q n t)").bitcast(F32).rearrange("p (n u) -> p n u", u=2),
+            in_=turned[:].rearrange("p u n -> p n u"),
+        )
 
         late = held.tile([P, 2, PASSES, P], U32, name="late", tag="dy_all1", align_bytes=64)
         codes_x = late[:, 0, :, :]

@@ -17,11 +17,11 @@ U16 = mybir.dt.uint16
 U8 = mybir.dt.uint8
 FP8X4 = mybir.dt.float8_e4m3fn_x4
 MULT = mybir.AluOpType.mult
+ADD = mybir.AluOpType.add
 COPY = mybir.ActivationFunctionType.Copy
 
 CHUNKS = ((0, 1536), (1536, 3072), (3072, 4096))
 LAST = 384
-SHARE = 512
 
 
 def tile_moe_bdw_lin_none_kernel(tc, xT, dyT, gate, offs, out):
@@ -69,7 +69,7 @@ def tile_moe_bdw_lin_none_kernel(tc, xT, dyT, gate, offs, out):
             turned = bank(b, [P, passes, 2, P])
             for q in range(passes):
                 for u in range(2):
-                    nc.tensor.transpose(turned[:, q, u, :], srcs[q].bitcast(F32)[:, u:256:2], identity[:])
+                    nc.tensor.transpose(turned[:, q, u, :], srcs[q][u], identity[:])
             nc.scalar.copy(
                 out=rows.rearrange("p q n t -> p (q n t)").bitcast(F32).rearrange("p (q n u) -> p q n u", q=passes, u=2),
                 in_=turned[:].rearrange("p q u n -> p q n u"),
@@ -94,11 +94,12 @@ def tile_moe_bdw_lin_none_kernel(tc, xT, dyT, gate, offs, out):
 
         for q in range(PASSES):
             gather_g(0, q * PASS, (q + 1) * PASS)
-        for part, (a, b) in zip(x_parts, CHUNKS):
+        for part, (a, b) in zip(x_parts[:-1], CHUNKS[:-1]):
             nc.scalar.copy(out=x_bf[:, a:b], in_=part[:])
+        nc.gpsimd.tensor_scalar(x_bf[:, CHUNKS[-1][0] :], x_parts[-1][:], 1.0, 0.0, MULT, ADD)
         rows_g0 = [
             held.tile([P, 2, P, 4], BF16, align_bytes=64, name="rows_g0a"),
-            held.tile([P, 2, P, 4], BF16, align_bytes=64, name="rows_g0b", tag=f"x_part{CHUNKS[-1][0]}"),
+            held.tile([P, 2, P, 4], BF16, align_bytes=64, name="rows_g0b", tag=f"x_part{CHUNKS[-2][0]}"),
         ]
         for q in range(PASSES):
             turn_g(0, q, 4 + q, rows_g0[q // 2][:, q % 2, :, :], nc.vector.tensor_copy if q < 2 else nc.scalar.copy)
@@ -106,14 +107,16 @@ def tile_moe_bdw_lin_none_kernel(tc, xT, dyT, gate, offs, out):
         early_x = first.tile([P, PASS], BF16, name="early_x", offset=0, align_bytes=64)
         later_x = first.tile([P, S - PASS], BF16, name="later_x", offset=4096, align_bytes=64)
         nc.vector.tensor_copy(early_x[:], x_bf[:].indirect(offsets[:, 0 : PASS // 16]))
-        nc.scalar.activation(later_x[:, SHARE - PASS :], x_bf[:].indirect(offsets[:, SHARE // 16 : S // 16]), COPY)
-        turn_words([early_x[:], later_x[:, 0:PASS]], rows_x[0][:], 0)
-        turn_words([later_x[:, PASS : 2 * PASS], later_x[:, 2 * PASS :]], rows_x[1][:], 1)
+        nc.scalar.activation(later_x[:].rearrange("p (u w e) -> p w u e", u=2, e=2), x_bf[:].indirect(offsets[:, PASS // 16 : S // 16]), COPY)
+        early_words = [early_x[:].bitcast(F32)[:, u:256:2] for u in range(2)]
+        later_words = [[later_x[:].bitcast(F32)[:, (3 * u + q) * P : (3 * u + q + 1) * P] for u in range(2)] for q in range(3)]
+        turn_words([early_words, later_words[0]], rows_x[0][:], 0)
+        turn_words([later_words[1], later_words[2]], rows_x[1][:], 1)
         codes_g0 = held.tile([P, PASSES, P], U32, name="codes_g0", align_bytes=64)
         for e in range(E):
             quantize(codes_g0[:, 2 * e : 2 * e + 2, :], scales_g[0][:, 2 * e * P : (2 * e + 2) * P], rows_g0[e][:])
 
-        picked_g.append(held.tile([P, S], F32, name="picked_g1", tag=f"x_part{CHUNKS[-1][0]}", align_bytes=64))
+        picked_g.append(held.tile([P, S], F32, name="picked_g1", tag=f"x_part{CHUNKS[-2][0]}", align_bytes=64))
         for q in range(3):
             gather_g(1, q * PASS, (q + 1) * PASS)
             turn_g(1, q, 3 + q, rows_g1[:, q, :, :], nc.scalar.copy)

@@ -20,148 +20,154 @@ MULT = mybir.AluOpType.mult
 ADD = mybir.AluOpType.add
 COPY = mybir.ActivationFunctionType.Copy
 
-CHUNKS = ((0, 1536), (1536, 3072), (3072, 4096))
-LAST = 384
-
 
 def tile_moe_bdw_lin_none_kernel(tc, xT, dyT, gate, offs, out):
     nc = tc.nc
     with ExitStack() as ctx:
         held = ctx.enter_context(tc.tile_pool(name="held", bufs=1))
-        first = ctx.enter_context(tc.tile_pool(name="first", bufs=1))
+        lap_b = ctx.enter_context(tc.tile_pool(name="lap_b", bufs=1))
         psum = ctx.enter_context(tc.psum_pool(name="psum", bufs=1))
 
         def bank(b, shape):
             return psum.tile(shape, F32, name=f"bank{b}", tag=f"bank{b}")
 
+        def sbuf(shape, dtype, name, tag=None):
+            return held.tile(shape, dtype, name=name, tag=tag or name, align_bytes=64)
+
         offsets = held.tile([P, S // 16], U16, name="offsets")
-        gate_runs = held.tile([P, 16], F32, name="gate_runs")
-        x_parts = [held.tile([P, b - a], F32, name=f"x_part{a}", tag=f"x_part{a}", align_bytes=64) for a, b in CHUNKS]
-        dy_all = [held.tile([P, T], F32, name="dy_all0"), held.tile([P, T], F32, name="dy_all1", tag="dy_all1", align_bytes=64)]
-        nc.sync.dma_start(gate_runs[:], gate[0:1, :].rearrange("o (k j) -> k (o j)", j=16))
+        gates = sbuf([P, PASSES, 4], F32, "gates")
+        dy_all = [held.tile([P, T], F32, name=f"dy_all{h}") for h in range(2)]
+        x_all = held.tile([P, T], F32, name="x_all")
+        nc.sync.dma_start(gates[:], gate[0:1, :].rearrange("o (q p t) -> p (o q) t", p=P, t=4))
         nc.sync.dma_start(offsets[:], offs)
-        nc.scalar.dma_start(dy_all[0][:], dyT[0:P, :])
-        for part, (a, b) in zip(x_parts, CHUNKS):
-            nc.scalar.dma_start(part[:], xT[:, a:b])
-        nc.scalar.dma_start(dy_all[1][:], dyT[P : 2 * P, :])
+        for h in range(2):
+            nc.scalar.dma_start(dy_all[h][:], dyT[h * P : (h + 1) * P, :])
+        nc.scalar.dma_start(x_all[:], xT)
 
         identity = held.tile([P, P], F32, name="identity")
         make_identity(nc, identity[:])
 
-        gates = held.tile([P, P, 16], F32, name="gates")
-        for b in range(4):
-            spread = bank(b, [P, 4, P])
-            for j in range(4):
-                nc.tensor.transpose(spread[:, j, :], gate_runs[:, 4 * b + j : 4 * b + j + 1].to_broadcast([P, P]), identity[:])
-            nc.vector.tensor_copy(gates[:, :, 4 * b : 4 * b + 4], spread[:].rearrange("p j k -> p k j"))
-
-        x_bf = held.tile([P, T], BF16, name="x_bf")
-        rows_x = [held.tile([P, 2, P, 4], BF16, align_bytes=64, name=f"rows_x{e}") for e in range(E)]
-        scales_x = held.tile([P, S // 4], U8, align_bytes=64, name="scales_x")
-        picked_g = [first.tile([P, S], F32, name="picked_g0", offset=0, align_bytes=64)]
-        rows_g1 = held.tile([P, PASSES, P, 4], BF16, align_bytes=64, name="rows_g1")
-        scales_g = [held.tile([P, S // 4], U8, align_bytes=64, name=f"scales_g{h}") for h in range(2)]
-        last_bf = held.tile([P, PASS], BF16, name="last_bf")
-        last_rows = held.tile([P, 1, P, 4], BF16, name="last_rows", align_bytes=64)
-
-        def turn_words(srcs, rows, b):
-            passes = len(srcs)
-            turned = bank(b, [P, passes, 2, P])
-            for q in range(passes):
-                for u in range(2):
-                    nc.tensor.transpose(turned[:, q, u, :], srcs[q][u], identity[:])
-            nc.scalar.copy(
-                out=rows.rearrange("p q n t -> p (q n t)").bitcast(F32).rearrange("p (q n u) -> p q n u", q=passes, u=2),
-                in_=turned[:].rearrange("p q u n -> p q n u"),
+        gate_row = held.tile([P, 2 * PASS], F32, name="gate_row")
+        for j in range(2):
+            spread = bank(6 + j, [P, 4, P])
+            for t in range(4):
+                nc.tensor.transpose(spread[:, t, :], gates[:, 2 + j, t : t + 1].to_broadcast([P, P]), identity[:])
+            nc.scalar.activation(
+                gate_row[:, j * PASS : (j + 1) * PASS].rearrange("p (k t) -> p k t", t=4), spread[:].rearrange("p t k -> p k t"), COPY
             )
+
+        codes_g = [sbuf([P, PASSES * P], U32, f"codes_g{h}") for h in range(2)]
+        scales_g = [sbuf([P, PASSES * P], U8, f"scales_g{h}") for h in range(2)]
+
+        def look_up(window, a, b):
+            return window[:].indirect(offsets[:, a // 16 : b // 16])
 
         def quantize(codes, scales, rows):
-            nc.vector.quantize_mx(
-                out=codes.rearrange("p q n -> p (q n)").bitcast(FP8X4),
-                scales=scales,
-                in_=rows.rearrange("p q n t -> p (q n t)"),
-            )
+            nc.vector.quantize_mx(out=codes.bitcast(FP8X4), scales=scales, in_=rows)
 
-        def gather_g(h, a, b):
-            gate_cols = gates[:].rearrange("p k j -> p (k j)")[:, a:b]
-            nc.vector.tensor_tensor(picked_g[h][:, a:b], dy_all[h][:].indirect(offsets[:, a // 16 : b // 16]), gate_cols, MULT)
-
-        def turn_g(h, q, b, rows, copy):
+        def turn_values(picked, q, b):
             turned = bank(b, [P, 4, P])
             for t in range(4):
-                nc.tensor.transpose(turned[:, t, :], picked_g[h][:, q * PASS + t : (q + 1) * PASS : 4], identity[:])
-            copy(out=rows, in_=turned[:].rearrange("p t n -> p n t"))
+                nc.tensor.transpose(turned[:, t, :], picked[:, q * PASS + t : (q + 1) * PASS : 4], identity[:])
+            return turned
 
-        for q in range(PASSES):
-            gather_g(0, q * PASS, (q + 1) * PASS)
-        for part, (a, b) in zip(x_parts[:-1], CHUNKS[:-1]):
-            nc.scalar.copy(out=x_bf[:, a:b], in_=part[:])
-        nc.gpsimd.tensor_scalar(x_bf[:, CHUNKS[-1][0] :], x_parts[-1][:], 1.0, 0.0, MULT, ADD)
-        rows_g0 = [
-            held.tile([P, 2, P, 4], BF16, align_bytes=64, name="rows_g0a"),
-            held.tile([P, 2, P, 4], BF16, align_bytes=64, name="rows_g0b", tag=f"x_part{CHUNKS[-2][0]}"),
-        ]
-        for q in range(PASSES):
-            turn_g(0, q, 4 + q, rows_g0[q // 2][:, q % 2, :, :], nc.vector.tensor_copy if q < 2 else nc.scalar.copy)
+        def gate_and_round(rows, gate_words, turned):
+            nc.vector.tensor_tensor(
+                rows.rearrange("p (n t) -> p n t", t=4),
+                turned[:].rearrange("p t n -> p n t"),
+                gate_words.to_broadcast([P, P, 4]),
+                MULT,
+            )
 
-        early_x = first.tile([P, PASS], BF16, name="early_x", offset=0, align_bytes=64)
-        later_x = first.tile([P, S - PASS], BF16, name="later_x", offset=4096, align_bytes=64)
-        nc.vector.tensor_copy(early_x[:], x_bf[:].indirect(offsets[:, 0 : PASS // 16]))
-        nc.scalar.activation(later_x[:].rearrange("p (u w e) -> p w u e", u=2, e=2), x_bf[:].indirect(offsets[:, PASS // 16 : S // 16]), COPY)
-        early_words = [early_x[:].bitcast(F32)[:, u:256:2] for u in range(2)]
-        later_words = [[later_x[:].bitcast(F32)[:, (3 * u + q) * P : (3 * u + q + 1) * P] for u in range(2)] for q in range(3)]
-        turn_words([early_words, later_words[0]], rows_x[0][:], 0)
-        turn_words([later_words[1], later_words[2]], rows_x[1][:], 1)
-        codes_g0 = held.tile([P, PASSES, P], U32, name="codes_g0", align_bytes=64)
+        def pairs_out(copy, rows, pair):
+            copy(out=rows.bitcast(F32).rearrange("p (q k u) -> p q k u", q=2, u=2), in_=pair[:].rearrange("p q u k -> p q k u"))
+
+        def turn_pairs(turned, rounded):
+            for u in range(2):
+                nc.tensor.transpose(turned[:, u, :], rounded.bitcast(F32)[:, u:256:2], identity[:])
+
+        early1 = sbuf([P, 2 * PASS], F32, "early1")
+        nc.vector.tensor_copy(early1[:, 510:514], gates[:, 1, :])
+        even_x = sbuf([P, 2 * PASS], BF16, "even_x")[:]
+        nc.vector.tensor_copy(even_x.bitcast(F32)[:, 254:258], gates[:, 1, :])
+        early = sbuf([P, 2 * PASS], F32, "early0")
+        other = sbuf([P, 2 * PASS], F32, "other0")
+        nc.vector.tensor_copy(early[:, 0:256], look_up(dy_all[0], 0, 256))
+        nc.scalar.activation(early[:, 256:512], look_up(dy_all[0], 256, 512), COPY)
+        nc.vector.tensor_copy(other[:, 0:512], look_up(dy_all[0], 1024, 1536))
+        nc.scalar.activation(early[:, 512:1024], look_up(dy_all[0], 512, 1024), COPY)
+        nc.vector.tensor_copy(other[:, 512:768], look_up(dy_all[0], 1536, 1792))
+        nc.scalar.activation(other[:, 768:1024], look_up(dy_all[0], 1792, S), COPY)
+        rounded = [sbuf([P, PASS], BF16, f"rounded0{j}") for j in range(2)]
+        for j in range(2):
+            nc.gpsimd.tensor_tensor(rounded[j][:], other[:, j * PASS : (j + 1) * PASS], gate_row[:, j * PASS : (j + 1) * PASS], MULT)
+        turned = [turn_values(early, q, q) for q in range(2)]
+        rows_0 = lap_b.tile([P, S], BF16, name="rows_g0", offset=0, align_bytes=64)
+        gate_and_round(rows_0[:, 0:PASS], gates[:, 0:1, :], turned[0])
+        gate_and_round(rows_0[:, PASS : 2 * PASS], early1[:, 510:514].unsqueeze(1), turned[1])
+        pairs = bank(0, [P, 2, 2, P])
+        for j in range(2):
+            turn_pairs(pairs[:, j, :, :], rounded[j][:])
+
+        other = sbuf([P, 2 * PASS], F32, "other1", tag="rounded01")
+        nc.scalar.activation(early1[:, 0:256], look_up(dy_all[1], 0, 256), COPY)
+        nc.vector.tensor_copy(early1[:, 256:512], look_up(dy_all[1], 256, 512))
+        nc.vector.tensor_copy(early1[:, 512:1024], look_up(dy_all[1], 512, 1024))
+        pairs_out(nc.scalar.copy, rows_0[:, 2 * PASS :], pairs)
+        for j in range(2):
+            nc.scalar.activation(other[:, j * PASS : (j + 1) * PASS], look_up(dy_all[1], (2 + j) * PASS, (3 + j) * PASS), COPY)
+        quantize(codes_g[0][:], scales_g[0][:], rows_0[:])
+        turned = [turn_values(early1, q, 4 + q) for q in range(2)]
+        rows_1 = lap_b.tile([P, S], BF16, name="rows_g1", offset=3072, align_bytes=64)
+        gate_and_round(rows_1[:, 0:PASS], gates[:, 0:1, :], turned[0])
+        rounded = [lap_b.tile([P, PASS], BF16, name="rounded10", offset=0, align_bytes=64), sbuf([P, PASS], BF16, "rounded11")]
+        for j in range(2):
+            nc.gpsimd.tensor_tensor(rounded[j][:], other[:, j * PASS : (j + 1) * PASS], gate_row[:, j * PASS : (j + 1) * PASS], MULT)
+        gate_and_round(rows_1[:, PASS : 2 * PASS], even_x.bitcast(F32)[:, 254:258].unsqueeze(1), turned[1])
+        pairs = bank(5, [P, 2, 2, P])
+        for j in range(2):
+            turn_pairs(pairs[:, j, :, :], rounded[j][:])
+
+        odd_x = lap_b.tile([P, 2 * PASS], BF16, name="odd_x", offset=1024, align_bytes=64)[:]
+        nc.vector.tensor_copy(even_x[:, 0:512], look_up(x_all, 0, 512))
+        nc.scalar.activation(odd_x[:, 0:512], look_up(x_all, 512, 1024), COPY)
+        nc.scalar.activation(odd_x[:, 512:1024], look_up(x_all, 1536, S), COPY)
+        nc.vector.tensor_copy(even_x[:, 512:1024], look_up(x_all, 1024, 1536))
+        pairs_out(nc.vector.tensor_copy, rows_1[:, 2 * PASS :], pairs)
+        quantize(codes_g[1][:], scales_g[1][:], rows_1[:])
+
+        def turn_words(turned, q):
+            words = (even_x, odd_x)[q % 2].bitcast(F32)
+            for u in range(2):
+                nc.tensor.transpose(turned[:, u, :], words[:, (q // 2) * 256 + u : (q // 2 + 1) * 256 : 2], identity[:])
+
+        codes_x = sbuf([P, PASSES * K], U32, "codes_x")
+        scales_x = sbuf([P, PASSES * K], U8, "scales_x")
         for e in range(E):
-            quantize(codes_g0[:, 2 * e : 2 * e + 2, :], scales_g[0][:, 2 * e * P : (2 * e + 2) * P], rows_g0[e][:])
+            pair = bank(2 + e, [P, 2, 2, P])
+            for j in (1, 0):
+                turn_words(pair[:, j, :, :], 2 * e + j)
+            rows = sbuf([P, 2 * PASS], BF16, f"rows_x{e}")
+            pairs_out(nc.scalar.copy, rows[:], pair)
+            quantize(codes_x[:, 2 * e * K : (2 * e + 2) * K], scales_x[:, 2 * e * K : (2 * e + 2) * K], rows[:])
 
-        picked_g.append(held.tile([P, S], F32, name="picked_g1", tag=f"x_part{CHUNKS[-2][0]}", align_bytes=64))
-        for q in range(3):
-            gather_g(1, q * PASS, (q + 1) * PASS)
-            turn_g(1, q, 3 + q, rows_g1[:, q, :, :], nc.scalar.copy)
-        gather_g(1, 1536, 1536 + LAST)
-        gather_g(1, 1536 + LAST, S)
-        last_halves = last_bf[:].rearrange("p (u w e) -> p u w e", u=2, e=2)
-        for a, b in ((0, LAST), (LAST, PASS)):
-            nc.vector.tensor_copy(
-                last_halves[:, :, a // 4 : b // 4, :],
-                picked_g[1][:, 1536 + a : 1536 + b].rearrange("p (w u e) -> p u w e", u=2, e=2),
-            )
-        turned = bank(6, [P, 2, P])
-        for u in range(2):
-            nc.tensor.transpose(turned[:, u, :], last_bf[:].bitcast(F32)[:, u * P : (u + 1) * P], identity[:])
-        nc.scalar.copy(
-            out=last_rows[:].rearrange("p q n t -> p (q n t)").bitcast(F32).rearrange("p (n u) -> p n u", u=2),
-            in_=turned[:].rearrange("p u n -> p n u"),
-        )
-
-        late = held.tile([P, 2, PASSES, P], U32, name="late", tag="dy_all1", align_bytes=64)
-        codes_x = late[:, 0, :, :]
-        codes_g = [codes_g0[:], late[:, 1, :, :]]
-        quantize(codes_x[:, 2:4, :], scales_x[:, 2 * P : 4 * P], rows_x[1][:])
-        quantize(codes_x[:, 0:2, :], scales_x[:, 0 : 2 * P], rows_x[0][:])
-        quantize(codes_g[1][:, 0:2, :], scales_g[1][:, 0 : 2 * P], rows_g1[:, 0:2, :, :])
-        quantize(codes_g[1][:, 2:3, :], scales_g[1][:, 2 * P : 3 * P], rows_g1[:, 2:3, :, :])
-        quantize(codes_g[1][:, 3:4, :], scales_g[1][:, 3 * P : 4 * P], last_rows[:])
-
-        accs = {(0, 1): bank(7, [P, P]), (1, 1): bank(0, [P, P]), (0, 0): bank(1, [P, P]), (1, 0): bank(2, [P, P])}
-        for h, q in ((0, 2), (0, 3), (0, 0), (0, 1), (1, 0), (1, 1), (1, 2), (1, 3)):
+        accs = {(0, 0): bank(1, [P, P]), (0, 1): bank(0, [P, P]), (1, 0): bank(6, [P, P]), (1, 1): bank(7, [P, P])}
+        for q, h in ((0, 0), (1, 0), (0, 1), (1, 1), (3, 0), (2, 0), (3, 1), (2, 1)):
             e = q // 2
-            cols = slice(q * P, (q + 1) * P)
+            closes = q in (1, 2)
             nc.tensor.matmul_mx(
-                out=accs[h, e][:],
-                lhsT=codes_x[:, q, :].bitcast(FP8X4),
-                lhsT_scale=scales_x[:, cols],
-                rhs=codes_g[h][:, q, :].bitcast(FP8X4),
-                rhs_scale=scales_g[h][:, cols],
-                start=(q % 2 == 0),
-                stop=(q % 2 == 1),
+                out=accs[e, h][:],
+                lhsT=codes_x[:, q * K : (q + 1) * K].bitcast(FP8X4),
+                lhsT_scale=scales_x[:, q * K : (q + 1) * K],
+                rhs=codes_g[h][:, q * P : (q + 1) * P].bitcast(FP8X4),
+                rhs_scale=scales_g[h][:, q * P : (q + 1) * P],
+                start=not closes,
+                stop=closes,
             )
-            if q % 2 == 1:
-                res = held.tile([P, P], F32, name=f"res{h}{e}")
-                if (h, q) == (1, 3):
-                    nc.vector.tensor_copy(res[:], accs[h, e][:])
+            if closes:
+                res = held.tile([P, P], F32, name=f"res{e}{h}")
+                if (e, h) == (1, 1):
+                    nc.vector.tensor_copy(res[:], accs[e, h][:])
                 else:
-                    nc.scalar.copy(out=res[:], in_=accs[h, e][:])
+                    nc.scalar.copy(out=res[:], in_=accs[e, h][:])
                 nc.sync.dma_start(out[e, :, h * P : (h + 1) * P], res[:])

@@ -56,14 +56,17 @@ def tile_moe_bdw_lin_none_kernel(tc, xT, dyT, gate, offs, out):
                 gate_row[:, j * PASS : (j + 1) * PASS].rearrange("p (k t) -> p k t", t=4), spread[:].rearrange("p t k -> p k t"), COPY
             )
 
-        codes_g = [sbuf([P, PASSES * P], U32, f"codes_g{h}") for h in range(2)]
-        scales_g = [sbuf([P, PASSES * P], U8, f"scales_g{h}") for h in range(2)]
+        codes_g = sbuf([P, 2 * PASSES * P], U32, "codes_g")
+        scales_g = sbuf([P, 2 * PASSES * P], U8, "scales_g")
 
         def look_up(window, a, b):
             return window[:].indirect(offsets[:, a // 16 : b // 16])
 
         def quantize(codes, scales, rows):
             nc.vector.quantize_mx(out=codes.bitcast(FP8X4), scales=scales, in_=rows)
+
+        def quantize_g(a, b, rows):
+            quantize(codes_g[:, a * P : b * P], scales_g[:, a * P : b * P], rows)
 
         def turn_values(picked, q, b):
             turned = bank(b, [P, 4, P])
@@ -102,39 +105,41 @@ def tile_moe_bdw_lin_none_kernel(tc, xT, dyT, gate, offs, out):
         for j in range(2):
             nc.gpsimd.tensor_tensor(rounded[j][:], other[:, j * PASS : (j + 1) * PASS], gate_row[:, j * PASS : (j + 1) * PASS], MULT)
         turned = [turn_values(early, q, q) for q in range(2)]
-        rows_0 = lap_b.tile([P, S], BF16, name="rows_g0", offset=0, align_bytes=64)
-        gate_and_round(rows_0[:, 0:PASS], gates[:, 0:1, :], turned[0])
-        gate_and_round(rows_0[:, PASS : 2 * PASS], early1[:, 510:514].unsqueeze(1), turned[1])
+        rows_b0 = sbuf([P, 2 * PASS], BF16, "rows_b0")
+        rows_mid = lap_b.tile([P, 3 * PASS], BF16, name="rows_mid", offset=0, align_bytes=64)
+        gate_and_round(rows_b0[:, 0:PASS], gates[:, 0:1, :], turned[0])
+        gate_and_round(rows_b0[:, PASS:], early1[:, 510:514].unsqueeze(1), turned[1])
         pairs = bank(0, [P, 2, 2, P])
         for j in range(2):
             turn_pairs(pairs[:, j, :, :], rounded[j][:])
 
-        other = sbuf([P, 2 * PASS], F32, "other1", tag="rounded01")
+        other = [sbuf([P, PASS], F32, "other10"), sbuf([P, PASS], F32, "other11", tag="rounded01")]
         nc.scalar.activation(early1[:, 0:256], look_up(dy_all[1], 0, 256), COPY)
         nc.vector.tensor_copy(early1[:, 256:512], look_up(dy_all[1], 256, 512))
         nc.vector.tensor_copy(early1[:, 512:1024], look_up(dy_all[1], 512, 1024))
-        pairs_out(nc.scalar.copy, rows_0[:, 2 * PASS :], pairs)
-        for j in range(2):
-            nc.scalar.activation(other[:, j * PASS : (j + 1) * PASS], look_up(dy_all[1], (2 + j) * PASS, (3 + j) * PASS), COPY)
-        quantize(codes_g[0][:], scales_g[0][:], rows_0[:])
+        nc.scalar.activation(other[0][:], look_up(dy_all[1], 2 * PASS, 3 * PASS), COPY)
+        quantize_g(0, 2, rows_b0[:])
+        pairs_out(nc.scalar.copy, rows_mid[:, 0 : 2 * PASS], pairs)
+        nc.scalar.activation(other[1][:], look_up(dy_all[1], 3 * PASS, S), COPY)
         turned = [turn_values(early1, q, 4 + q) for q in range(2)]
-        rows_1 = lap_b.tile([P, S], BF16, name="rows_g1", offset=3072, align_bytes=64)
-        gate_and_round(rows_1[:, 0:PASS], gates[:, 0:1, :], turned[0])
-        rounded = [lap_b.tile([P, PASS], BF16, name="rounded10", offset=0, align_bytes=64), sbuf([P, PASS], BF16, "rounded11")]
+        gate_and_round(rows_mid[:, 2 * PASS :], gates[:, 0:1, :], turned[0])
+        quantize_g(2, 5, rows_mid[:])
+        rows_b1 = lap_b.tile([P, PASS], BF16, name="rows_b1", offset=0, align_bytes=64)
+        rows_w1 = sbuf([P, 2 * PASS], BF16, "rows_w1")
+        rounded = [sbuf([P, PASS], BF16, f"rounded1{j}") for j in range(2)]
         for j in range(2):
-            nc.gpsimd.tensor_tensor(rounded[j][:], other[:, j * PASS : (j + 1) * PASS], gate_row[:, j * PASS : (j + 1) * PASS], MULT)
-        gate_and_round(rows_1[:, PASS : 2 * PASS], even_x.bitcast(F32)[:, 254:258].unsqueeze(1), turned[1])
+            nc.gpsimd.tensor_tensor(rounded[j][:], other[j][:], gate_row[:, j * PASS : (j + 1) * PASS], MULT)
+        gate_and_round(rows_b1[:], even_x.bitcast(F32)[:, 254:258].unsqueeze(1), turned[1])
         pairs = bank(5, [P, 2, 2, P])
         for j in range(2):
             turn_pairs(pairs[:, j, :, :], rounded[j][:])
 
-        odd_x = lap_b.tile([P, 2 * PASS], BF16, name="odd_x", offset=1024, align_bytes=64)[:]
+        odd_x = lap_b.tile([P, 2 * PASS], BF16, name="odd_x", offset=2048, align_bytes=64)[:]
         nc.vector.tensor_copy(even_x[:, 0:512], look_up(x_all, 0, 512))
         nc.scalar.activation(odd_x[:, 0:512], look_up(x_all, 512, 1024), COPY)
         nc.scalar.activation(odd_x[:, 512:1024], look_up(x_all, 1536, S), COPY)
         nc.vector.tensor_copy(even_x[:, 512:1024], look_up(x_all, 1024, 1536))
-        pairs_out(nc.vector.tensor_copy, rows_1[:, 2 * PASS :], pairs)
-        quantize(codes_g[1][:], scales_g[1][:], rows_1[:])
+        pairs_out(nc.scalar.copy, rows_w1[:], pairs)
 
         def turn_words(turned, q):
             words = (even_x, odd_x)[q % 2].bitcast(F32)
@@ -143,24 +148,31 @@ def tile_moe_bdw_lin_none_kernel(tc, xT, dyT, gate, offs, out):
 
         codes_x = sbuf([P, PASSES * K], U32, "codes_x")
         scales_x = sbuf([P, PASSES * K], U8, "scales_x")
-        for e in range(E):
-            pair = bank(2 + e, [P, 2, 2, P])
-            for j in (1, 0):
-                turn_words(pair[:, j, :, :], 2 * e + j)
-            rows = sbuf([P, 2 * PASS], BF16, f"rows_x{e}")
-            pairs_out(nc.scalar.copy, rows[:], pair)
-            quantize(codes_x[:, 2 * e * K : (2 * e + 2) * K], scales_x[:, 2 * e * K : (2 * e + 2) * K], rows[:])
+        pair = bank(2, [P, 2, 2, P])
+        for j in (1, 0):
+            turn_words(pair[:, j, :, :], j)
+        rows = sbuf([P, 2 * PASS], BF16, "rows_x01")
+        pairs_out(nc.vector.tensor_copy, rows[:], pair)
+        quantize_g(5, 6, rows_b1[:])
+        quantize(codes_x[:, 0 : 2 * K], scales_x[:, 0 : 2 * K], rows[:])
+        quantize_g(6, 8, rows_w1[:])
+        for q, b in ((2, 3), (3, 1)):
+            single = bank(b, [P, 2, P])
+            turn_words(single, q)
+            rows = sbuf([P, PASS], BF16, f"rows_x{q}")
+            nc.scalar.copy(out=rows[:].bitcast(F32).rearrange("p (k u) -> p k u", u=2), in_=single[:].rearrange("p u k -> p k u"))
+            quantize(codes_x[:, q * K : (q + 1) * K], scales_x[:, q * K : (q + 1) * K], rows[:])
 
-        accs = {(0, 0): bank(1, [P, P]), (0, 1): bank(0, [P, P]), (1, 0): bank(6, [P, P]), (1, 1): bank(7, [P, P])}
-        for q, h in ((0, 0), (1, 0), (0, 1), (1, 1), (3, 0), (2, 0), (3, 1), (2, 1)):
+        accs = {(0, 0): bank(4, [P, P]), (0, 1): bank(0, [P, P]), (1, 0): bank(6, [P, P]), (1, 1): bank(7, [P, P])}
+        for q, h in ((0, 0), (1, 0), (0, 1), (1, 1), (2, 0), (2, 1), (3, 0), (3, 1)):
             e = q // 2
-            closes = q in (1, 2)
+            closes = q % 2 == 1
             nc.tensor.matmul_mx(
                 out=accs[e, h][:],
                 lhsT=codes_x[:, q * K : (q + 1) * K].bitcast(FP8X4),
                 lhsT_scale=scales_x[:, q * K : (q + 1) * K],
-                rhs=codes_g[h][:, q * P : (q + 1) * P].bitcast(FP8X4),
-                rhs_scale=scales_g[h][:, q * P : (q + 1) * P],
+                rhs=codes_g[:, (4 * h + q) * P : (4 * h + q + 1) * P].bitcast(FP8X4),
+                rhs_scale=scales_g[:, (4 * h + q) * P : (4 * h + q + 1) * P],
                 start=not closes,
                 stop=closes,
             )

@@ -91,8 +91,9 @@ def tile_moe_bdw_lin_none_kernel(tc, xT, dyT, gate, offs, out):
 
         early1 = sbuf([P, 2 * PASS], F32, "early1")
         nc.vector.tensor_copy(early1[:, 510:514], gates[:, 1, :])
-        even_x = sbuf([P, 2 * PASS], BF16, "even_x")[:]
-        nc.vector.tensor_copy(even_x.bitcast(F32)[:, 254:258], gates[:, 1, :])
+        even_x = sbuf([P, 1312], BF16, "even_x")[:]
+        last_gates = even_x.bitcast(F32)[:, 255:641].rearrange("p (a b) -> p a b", a=2)[:, :, 0:2]
+        nc.vector.tensor_copy(last_gates, gates[:, 1, :].rearrange("p (a b) -> p a b", a=2))
         early = sbuf([P, 2 * PASS], F32, "early0")
         other = sbuf([P, 2 * PASS], F32, "other0")
         nc.vector.tensor_copy(early[:, 0:256], look_up(dy_all[0], 0, 256))
@@ -129,7 +130,12 @@ def tile_moe_bdw_lin_none_kernel(tc, xT, dyT, gate, offs, out):
         rounded = [sbuf([P, PASS], BF16, f"rounded1{j}") for j in range(2)]
         for j in range(2):
             nc.gpsimd.tensor_tensor(rounded[j][:], other[j][:], gate_row[:, j * PASS : (j + 1) * PASS], MULT)
-        gate_and_round(rows_b1[:], even_x.bitcast(F32)[:, 254:258].unsqueeze(1), turned[1])
+        nc.vector.tensor_tensor(
+            rows_b1[:].rearrange("p (n a b) -> p n a b", a=2, b=2),
+            turned[1][:].rearrange("p (a b) n -> p n a b", a=2),
+            last_gates.unsqueeze(1).to_broadcast([P, P, 2, 2]),
+            MULT,
+        )
         pairs = bank(5, [P, 2, 2, P])
         for j in range(2):
             turn_pairs(pairs[:, j, :, :], rounded[j][:])
@@ -138,7 +144,8 @@ def tile_moe_bdw_lin_none_kernel(tc, xT, dyT, gate, offs, out):
         nc.vector.tensor_copy(even_x[:, 0:512], look_up(x_all, 0, 512))
         nc.scalar.activation(odd_x[:, 0:512], look_up(x_all, 512, 1024), COPY)
         nc.scalar.activation(odd_x[:, 512:1024], look_up(x_all, 1536, S), COPY)
-        nc.vector.tensor_copy(even_x[:, 512:1024], look_up(x_all, 1024, 1536))
+        nc.vector.tensor_copy(even_x[:, 512:896], look_up(x_all, 1024, 1408))
+        nc.scalar.activation(even_x[:, 896:1024], look_up(x_all, 1408, 1536), COPY)
         pairs_out(nc.scalar.copy, rows_w1[:], pairs)
 
         def turn_words(turned, q):
@@ -156,7 +163,7 @@ def tile_moe_bdw_lin_none_kernel(tc, xT, dyT, gate, offs, out):
         quantize_g(5, 6, rows_b1[:])
         quantize(codes_x[:, 0 : 2 * K], scales_x[:, 0 : 2 * K], rows[:])
         quantize_g(6, 8, rows_w1[:])
-        for q, b in ((2, 3), (3, 1)):
+        for q, b in ((3, 1), (2, 3)):
             single = bank(b, [P, 2, P])
             turn_words(single, q)
             rows = sbuf([P, PASS], BF16, f"rows_x{q}")
@@ -164,9 +171,9 @@ def tile_moe_bdw_lin_none_kernel(tc, xT, dyT, gate, offs, out):
             quantize(codes_x[:, q * K : (q + 1) * K], scales_x[:, q * K : (q + 1) * K], rows[:])
 
         accs = {(0, 0): bank(4, [P, P]), (0, 1): bank(0, [P, P]), (1, 0): bank(6, [P, P]), (1, 1): bank(7, [P, P])}
-        for q, h in ((0, 0), (1, 0), (0, 1), (1, 1), (2, 0), (2, 1), (3, 0), (3, 1)):
+        for q, h in ((0, 0), (1, 0), (0, 1), (1, 1), (3, 0), (3, 1), (2, 0), (2, 1)):
             e = q // 2
-            closes = q % 2 == 1
+            closes = q in (1, 2)
             nc.tensor.matmul_mx(
                 out=accs[e, h][:],
                 lhsT=codes_x[:, q * K : (q + 1) * K].bitcast(FP8X4),

@@ -25,7 +25,6 @@ def tile_moe_bdw_lin_none_kernel(tc, xT, dyT, gate, offs, out):
     nc = tc.nc
     with ExitStack() as ctx:
         held = ctx.enter_context(tc.tile_pool(name="held", bufs=1))
-        lap_b = ctx.enter_context(tc.tile_pool(name="lap_b", bufs=1))
         psum = ctx.enter_context(tc.psum_pool(name="psum", bufs=1))
 
         def bank(b, shape):
@@ -85,14 +84,17 @@ def tile_moe_bdw_lin_none_kernel(tc, xT, dyT, gate, offs, out):
         def pairs_out(copy, rows, pair):
             copy(out=rows.bitcast(F32).rearrange("p (q k u) -> p q k u", q=2, u=2), in_=pair[:].rearrange("p q u k -> p q k u"))
 
+        def words_out(copy, rows, single):
+            copy(out=rows.bitcast(F32).rearrange("p (k u) -> p k u", u=2), in_=single[:].rearrange("p u k -> p k u"))
+
         def turn_pairs(turned, rounded):
             for u in range(2):
                 nc.tensor.transpose(turned[:, u, :], rounded.bitcast(F32)[:, u:256:2], identity[:])
 
         early1 = sbuf([P, 2 * PASS], F32, "early1")
         nc.vector.tensor_copy(early1[:, 510:514], gates[:, 1, :])
-        even_x = sbuf([P, 1312], BF16, "even_x")[:]
-        last_gates = even_x.bitcast(F32)[:, 255:641].rearrange("p (a b) -> p a b", a=2)[:, :, 0:2]
+        even_x = sbuf([P, 1568], BF16, "even_x")[:]
+        last_gates = even_x.bitcast(F32)[:, 250:770].rearrange("p (a b c) -> p a b c", a=2, b=2)[:, :, :, 0]
         nc.vector.tensor_copy(last_gates, gates[:, 1, :].rearrange("p (a b) -> p a b", a=2))
         early = sbuf([P, 2 * PASS], F32, "early0")
         other = sbuf([P, 2 * PASS], F32, "other0")
@@ -100,58 +102,54 @@ def tile_moe_bdw_lin_none_kernel(tc, xT, dyT, gate, offs, out):
         nc.scalar.activation(early[:, 256:512], look_up(dy_all[0], 256, 512), COPY)
         nc.vector.tensor_copy(other[:, 0:512], look_up(dy_all[0], 1024, 1536))
         nc.scalar.activation(early[:, 512:1024], look_up(dy_all[0], 512, 1024), COPY)
-        nc.vector.tensor_copy(other[:, 512:768], look_up(dy_all[0], 1536, 1792))
-        nc.scalar.activation(other[:, 768:1024], look_up(dy_all[0], 1792, S), COPY)
+        nc.scalar.activation(other[:, 512:1024], look_up(dy_all[0], 1536, S), COPY)
         rounded = [sbuf([P, PASS], BF16, f"rounded0{j}") for j in range(2)]
         for j in range(2):
             nc.gpsimd.tensor_tensor(rounded[j][:], other[:, j * PASS : (j + 1) * PASS], gate_row[:, j * PASS : (j + 1) * PASS], MULT)
         turned = [turn_values(early, q, q) for q in range(2)]
         rows_b0 = sbuf([P, 2 * PASS], BF16, "rows_b0")
-        rows_mid = lap_b.tile([P, 3 * PASS], BF16, name="rows_mid", offset=0, align_bytes=64)
+        rows_mid = sbuf([P, 4 * PASS], BF16, "rows_mid")
         gate_and_round(rows_b0[:, 0:PASS], gates[:, 0:1, :], turned[0])
         gate_and_round(rows_b0[:, PASS:], early1[:, 510:514].unsqueeze(1), turned[1])
         pairs = bank(0, [P, 2, 2, P])
         for j in range(2):
             turn_pairs(pairs[:, j, :, :], rounded[j][:])
 
-        other = [sbuf([P, PASS], F32, "other10"), sbuf([P, PASS], F32, "other11", tag="rounded01")]
+        other = sbuf([P, 2 * PASS], F32, "other1")
         nc.scalar.activation(early1[:, 0:256], look_up(dy_all[1], 0, 256), COPY)
         nc.vector.tensor_copy(early1[:, 256:512], look_up(dy_all[1], 256, 512))
         nc.vector.tensor_copy(early1[:, 512:1024], look_up(dy_all[1], 512, 1024))
-        nc.scalar.activation(other[0][:], look_up(dy_all[1], 2 * PASS, 3 * PASS), COPY)
+        for j in range(2):
+            nc.scalar.activation(other[:, j * PASS : (j + 1) * PASS], look_up(dy_all[1], (2 + j) * PASS, (3 + j) * PASS), COPY)
         quantize_g(0, 2, rows_b0[:])
         pairs_out(nc.scalar.copy, rows_mid[:, 0 : 2 * PASS], pairs)
-        nc.scalar.activation(other[1][:], look_up(dy_all[1], 3 * PASS, S), COPY)
         turned = [turn_values(early1, q, 4 + q) for q in range(2)]
-        gate_and_round(rows_mid[:, 2 * PASS :], gates[:, 0:1, :], turned[0])
-        quantize_g(2, 5, rows_mid[:])
-        rows_b1 = lap_b.tile([P, PASS], BF16, name="rows_b1", offset=0, align_bytes=64)
+        gate_and_round(rows_mid[:, 2 * PASS : 3 * PASS], gates[:, 0:1, :], turned[0])
         rows_w1 = sbuf([P, 2 * PASS], BF16, "rows_w1")
         rounded = [sbuf([P, PASS], BF16, f"rounded1{j}") for j in range(2)]
         for j in range(2):
-            nc.gpsimd.tensor_tensor(rounded[j][:], other[j][:], gate_row[:, j * PASS : (j + 1) * PASS], MULT)
+            nc.gpsimd.tensor_tensor(rounded[j][:], other[:, j * PASS : (j + 1) * PASS], gate_row[:, j * PASS : (j + 1) * PASS], MULT)
         nc.vector.tensor_tensor(
-            rows_b1[:].rearrange("p (n a b) -> p n a b", a=2, b=2),
+            rows_mid[:, 3 * PASS :].rearrange("p (n a b) -> p n a b", a=2, b=2),
             turned[1][:].rearrange("p (a b) n -> p n a b", a=2),
             last_gates.unsqueeze(1).to_broadcast([P, P, 2, 2]),
             MULT,
         )
-        pairs = bank(5, [P, 2, 2, P])
+        singles = [bank(4 + j, [P, 2, P]) for j in range(2)]
         for j in range(2):
-            turn_pairs(pairs[:, j, :, :], rounded[j][:])
+            turn_pairs(singles[j], rounded[j][:])
+        words_out(nc.vector.tensor_copy, rows_w1[:, 0:PASS], singles[0])
 
-        odd_x = lap_b.tile([P, 2 * PASS], BF16, name="odd_x", offset=2048, align_bytes=64)[:]
+        odd_x = sbuf([P, PASS], BF16, "odd_x", tag="early1")[:]
         nc.vector.tensor_copy(even_x[:, 0:512], look_up(x_all, 0, 512))
         nc.scalar.activation(odd_x[:, 0:512], look_up(x_all, 512, 1024), COPY)
-        nc.scalar.activation(odd_x[:, 512:1024], look_up(x_all, 1536, S), COPY)
-        nc.vector.tensor_copy(even_x[:, 512:896], look_up(x_all, 1024, 1408))
-        nc.scalar.activation(even_x[:, 896:1024], look_up(x_all, 1408, 1536), COPY)
-        pairs_out(nc.scalar.copy, rows_w1[:], pairs)
+        nc.scalar.activation(even_x[:, 1024:1536], look_up(x_all, 1536, S), COPY)
+        nc.vector.tensor_copy(even_x[:, 512:768], look_up(x_all, 1024, 1280))
+        nc.scalar.activation(even_x[:, 768:1024], look_up(x_all, 1280, 1536), COPY)
+        words_out(nc.scalar.copy, rows_w1[:, PASS:], singles[1])
 
         def turn_words(turned, q):
-            words = (even_x, odd_x)[q % 2].bitcast(F32)
-            for u in range(2):
-                nc.tensor.transpose(turned[:, u, :], words[:, (q // 2) * 256 + u : (q // 2 + 1) * 256 : 2], identity[:])
+            turn_pairs(turned, (even_x[:, 0:PASS], odd_x, even_x[:, PASS : 2 * PASS], even_x[:, 2 * PASS : 3 * PASS])[q])
 
         codes_x = sbuf([P, PASSES * K], U32, "codes_x")
         scales_x = sbuf([P, PASSES * K], U8, "scales_x")
@@ -160,17 +158,21 @@ def tile_moe_bdw_lin_none_kernel(tc, xT, dyT, gate, offs, out):
             turn_words(pair[:, j, :, :], j)
         rows = sbuf([P, 2 * PASS], BF16, "rows_x01")
         pairs_out(nc.vector.tensor_copy, rows[:], pair)
-        quantize_g(5, 6, rows_b1[:])
+        quantize_g(4, 6, rows_mid[:, 2 * PASS :])
+        codes_mid = sbuf([P, 2 * P], U32, "codes_mid", tag="rounded10")[:]
+        quantize(codes_mid, scales_g[:, 2 * P : 4 * P], rows_mid[:, 0 : 2 * PASS])
         quantize(codes_x[:, 0 : 2 * K], scales_x[:, 0 : 2 * K], rows[:])
         quantize_g(6, 8, rows_w1[:])
         for q, b in ((3, 1), (2, 3)):
             single = bank(b, [P, 2, P])
             turn_words(single, q)
             rows = sbuf([P, PASS], BF16, f"rows_x{q}")
-            nc.scalar.copy(out=rows[:].bitcast(F32).rearrange("p (k u) -> p k u", u=2), in_=single[:].rearrange("p u k -> p k u"))
+            words_out(nc.scalar.copy, rows[:], single)
             quantize(codes_x[:, q * K : (q + 1) * K], scales_x[:, q * K : (q + 1) * K], rows[:])
 
-        accs = {(0, 0): bank(4, [P, P]), (0, 1): bank(0, [P, P]), (1, 0): bank(6, [P, P]), (1, 1): bank(7, [P, P])}
+        words_g = [codes_g[:, i * P : (i + 1) * P] for i in range(2 * PASSES)]
+        words_g[2:4] = [codes_mid[:, 0:P], codes_mid[:, P:]]
+        accs = {(0, 0): bank(2, [P, P]), (0, 1): bank(0, [P, P]), (1, 0): bank(6, [P, P]), (1, 1): bank(7, [P, P])}
         for q, h in ((0, 0), (1, 0), (0, 1), (1, 1), (3, 0), (3, 1), (2, 0), (2, 1)):
             e = q // 2
             closes = q in (1, 2)
@@ -178,7 +180,7 @@ def tile_moe_bdw_lin_none_kernel(tc, xT, dyT, gate, offs, out):
                 out=accs[e, h][:],
                 lhsT=codes_x[:, q * K : (q + 1) * K].bitcast(FP8X4),
                 lhsT_scale=scales_x[:, q * K : (q + 1) * K],
-                rhs=codes_g[:, (4 * h + q) * P : (4 * h + q + 1) * P].bitcast(FP8X4),
+                rhs=words_g[4 * h + q].bitcast(FP8X4),
                 rhs_scale=scales_g[:, (4 * h + q) * P : (4 * h + q + 1) * P],
                 start=not closes,
                 stop=closes,

@@ -25,6 +25,7 @@ def tile_moe_bdw_lin_none_kernel(tc, xT, dyT, gate, offs, out):
     nc = tc.nc
     with ExitStack() as ctx:
         held = ctx.enter_context(tc.tile_pool(name="held", bufs=1))
+        lap = ctx.enter_context(tc.tile_pool(name="lap", bufs=1))
         psum = ctx.enter_context(tc.psum_pool(name="psum", bufs=1))
 
         def bank(b, shape):
@@ -34,10 +35,11 @@ def tile_moe_bdw_lin_none_kernel(tc, xT, dyT, gate, offs, out):
             return held.tile(shape, dtype, name=name, tag=tag or name, align_bytes=64)
 
         offsets = held.tile([P, S // 16], U16, name="offsets")
-        gates = sbuf([P, PASSES, 4], F32, "gates")
+        gates = sbuf([P, 2, 4], F32, "gates")
         dy_all = [held.tile([P, T], F32, name=f"dy_all{h}") for h in range(2)]
         x_all = held.tile([P, T], F32, name="x_all")
-        nc.sync.dma_start(gates[:], gate[0:1, :].rearrange("o (q p t) -> p (o q) t", p=P, t=4))
+        gate_runs = held.tile([P, 16], F32, name="gate_runs")
+        nc.sync.dma_start(gate_runs[:], gate[0:1, :].rearrange("o (k j) -> k (o j)", j=16))
         nc.sync.dma_start(offsets[:], offs)
         for h in range(2):
             nc.scalar.dma_start(dy_all[h][:], dyT[h * P : (h + 1) * P, :])
@@ -46,14 +48,23 @@ def tile_moe_bdw_lin_none_kernel(tc, xT, dyT, gate, offs, out):
         identity = held.tile([P, P], F32, name="identity")
         make_identity(nc, identity[:])
 
-        gate_row = held.tile([P, 2 * PASS], F32, name="gate_row")
-        for j in range(2):
-            spread = bank(6 + j, [P, 4, P])
+        by_place = lap.tile([P, 4, PASS], F32, name="by_place", offset=8192, align_bytes=64)
+        for t in range(4):
+            spread = bank(4 + t, [P, 4, P])
+            for r in range(4):
+                nc.tensor.transpose(spread[:, r, :], gate_runs[:, 4 * r + t : 4 * r + t + 1].to_broadcast([P, P]), identity[:])
+            places = by_place[:, t, :].rearrange("p (k r) -> p k r", r=4)
+            if t % 2 == 0:
+                nc.scalar.activation(places, spread[:].rearrange("p r k -> p k r"), COPY)
+            else:
+                nc.vector.tensor_copy(places, spread[:].rearrange("p r k -> p k r"))
+        for q in range(2):
+            back = bank(2 + q, [P, 4, P])
             for t in range(4):
-                nc.tensor.transpose(spread[:, t, :], gates[:, 2 + j, t : t + 1].to_broadcast([P, P]), identity[:])
-            nc.scalar.activation(
-                gate_row[:, j * PASS : (j + 1) * PASS].rearrange("p (k t) -> p k t", t=4), spread[:].rearrange("p t k -> p k t"), COPY
-            )
+                nc.tensor.transpose(back[:, t, :], by_place[:, t, q * P : (q + 1) * P], identity[:])
+            nc.vector.tensor_copy(gates[:, q, :], back[:, :, 0])
+        gate_row = held.tile([P, 2 * PASS], F32, name="gate_row")
+        nc.vector.tensor_copy(gate_row[:].rearrange("p (s t) -> p s t", t=4), by_place[:, :, 2 * P :].rearrange("p t s -> p s t"))
 
         codes_g = sbuf([P, 2 * PASSES * P], U32, "codes_g")
         scales_g = sbuf([P, 2 * PASSES * P], U8, "scales_g")
@@ -91,13 +102,14 @@ def tile_moe_bdw_lin_none_kernel(tc, xT, dyT, gate, offs, out):
             for u in range(2):
                 nc.tensor.transpose(turned[:, u, :], rounded.bitcast(F32)[:, u:256:2], identity[:])
 
-        early1 = sbuf([P, 2 * PASS], F32, "early1")
+        early1 = lap.tile([P, 2 * PASS], F32, name="early1", offset=14336, align_bytes=64)
         nc.vector.tensor_copy(early1[:, 510:514], gates[:, 1, :])
         even_x = sbuf([P, 1568], BF16, "even_x")[:]
         last_gates = even_x.bitcast(F32)[:, 250:770].rearrange("p (a b c) -> p a b c", a=2, b=2)[:, :, :, 0]
         nc.vector.tensor_copy(last_gates, gates[:, 1, :].rearrange("p (a b) -> p a b", a=2))
-        early = sbuf([P, 2 * PASS], F32, "early0")
-        other = sbuf([P, 2 * PASS], F32, "other0")
+        raw_0 = lap.tile([P, S], F32, name="raw_0", offset=2048, align_bytes=64)
+        early = raw_0[:, 0 : 2 * PASS]
+        other = raw_0[:, 2 * PASS :]
         nc.vector.tensor_copy(early[:, 0:256], look_up(dy_all[0], 0, 256))
         nc.scalar.activation(early[:, 256:512], look_up(dy_all[0], 256, 512), COPY)
         nc.vector.tensor_copy(other[:, 0:512], look_up(dy_all[0], 1024, 1536))
@@ -115,7 +127,7 @@ def tile_moe_bdw_lin_none_kernel(tc, xT, dyT, gate, offs, out):
         for j in range(2):
             turn_pairs(pairs[:, j, :, :], rounded[j][:])
 
-        other = sbuf([P, 2 * PASS], F32, "other1")
+        other = lap.tile([P, 2 * PASS], F32, name="other1", offset=10240, align_bytes=64)
         nc.scalar.activation(early1[:, 0:256], look_up(dy_all[1], 0, 256), COPY)
         nc.vector.tensor_copy(early1[:, 256:512], look_up(dy_all[1], 256, 512))
         nc.vector.tensor_copy(early1[:, 512:1024], look_up(dy_all[1], 512, 1024))
@@ -140,12 +152,12 @@ def tile_moe_bdw_lin_none_kernel(tc, xT, dyT, gate, offs, out):
             turn_pairs(singles[j], rounded[j][:])
         words_out(nc.vector.tensor_copy, rows_w1[:, 0:PASS], singles[0])
 
-        odd_x = sbuf([P, PASS], BF16, "odd_x", tag="early1")[:]
+        odd_x = lap.tile([P, PASS], BF16, name="odd_x", offset=16384, align_bytes=64)[:]
         nc.vector.tensor_copy(even_x[:, 0:512], look_up(x_all, 0, 512))
         nc.scalar.activation(odd_x[:, 0:512], look_up(x_all, 512, 1024), COPY)
         nc.scalar.activation(even_x[:, 1024:1536], look_up(x_all, 1536, S), COPY)
-        nc.vector.tensor_copy(even_x[:, 512:768], look_up(x_all, 1024, 1280))
-        nc.scalar.activation(even_x[:, 768:1024], look_up(x_all, 1280, 1536), COPY)
+        nc.vector.tensor_copy(even_x[:, 512:896], look_up(x_all, 1024, 1408))
+        nc.scalar.activation(even_x[:, 896:1024], look_up(x_all, 1408, 1536), COPY)
         words_out(nc.scalar.copy, rows_w1[:, PASS:], singles[1])
 
         def turn_words(turned, q):
@@ -158,9 +170,7 @@ def tile_moe_bdw_lin_none_kernel(tc, xT, dyT, gate, offs, out):
             turn_words(pair[:, j, :, :], j)
         rows = sbuf([P, 2 * PASS], BF16, "rows_x01")
         pairs_out(nc.vector.tensor_copy, rows[:], pair)
-        quantize_g(4, 6, rows_mid[:, 2 * PASS :])
-        codes_mid = sbuf([P, 2 * P], U32, "codes_mid", tag="rounded10")[:]
-        quantize(codes_mid, scales_g[:, 2 * P : 4 * P], rows_mid[:, 0 : 2 * PASS])
+        quantize_g(2, 6, rows_mid[:])
         quantize(codes_x[:, 0 : 2 * K], scales_x[:, 0 : 2 * K], rows[:])
         quantize_g(6, 8, rows_w1[:])
         for q, b in ((3, 1), (2, 3)):
@@ -171,7 +181,6 @@ def tile_moe_bdw_lin_none_kernel(tc, xT, dyT, gate, offs, out):
             quantize(codes_x[:, q * K : (q + 1) * K], scales_x[:, q * K : (q + 1) * K], rows[:])
 
         words_g = [codes_g[:, i * P : (i + 1) * P] for i in range(2 * PASSES)]
-        words_g[2:4] = [codes_mid[:, 0:P], codes_mid[:, P:]]
         accs = {(0, 0): bank(2, [P, P]), (0, 1): bank(0, [P, P]), (1, 0): bank(6, [P, P]), (1, 1): bank(7, [P, P])}
         for q, h in ((0, 0), (1, 0), (0, 1), (1, 1), (3, 0), (3, 1), (2, 0), (2, 1)):
             e = q // 2

@@ -58,11 +58,10 @@ def tile_moe_bdw_lin_none_kernel(tc, xT, dyT, gate, offs, out):
                 nc.scalar.activation(places, spread[:].rearrange("p r k -> p k r"), COPY)
             else:
                 nc.vector.tensor_copy(places, spread[:].rearrange("p r k -> p k r"))
-        for q in range(2):
-            back = bank(2 + q, [P, 4, P])
-            for t in range(4):
-                nc.tensor.transpose(back[:, t, :], by_place[:, t, q * P : (q + 1) * P], identity[:])
-            nc.vector.tensor_copy(gates[:, q, :], back[:, :, 0])
+        backs = [bank(2 + q, [P, 4, P]) for q in range(2)]
+        for t in range(4):
+            for q in range(2):
+                nc.tensor.transpose(backs[q][:, t, :], by_place[:, t, q * P : (q + 1) * P], identity[:])
         gate_row = held.tile([P, 2 * PASS], F32, name="gate_row")
         nc.vector.tensor_copy(gate_row[:].rearrange("p (s t) -> p s t", t=4), by_place[:, :, 2 * P :].rearrange("p t s -> p s t"))
 
@@ -103,10 +102,8 @@ def tile_moe_bdw_lin_none_kernel(tc, xT, dyT, gate, offs, out):
                 nc.tensor.transpose(turned[:, u, :], rounded.bitcast(F32)[:, u:256:2], identity[:])
 
         early1 = lap.tile([P, 2 * PASS], F32, name="early1", offset=14336, align_bytes=64)
-        nc.vector.tensor_copy(early1[:, 510:514], gates[:, 1, :])
         even_x = sbuf([P, 1568], BF16, "even_x")[:]
         last_gates = even_x.bitcast(F32)[:, 250:770].rearrange("p (a b c) -> p a b c", a=2, b=2)[:, :, :, 0]
-        nc.vector.tensor_copy(last_gates, gates[:, 1, :].rearrange("p (a b) -> p a b", a=2))
         raw_0 = lap.tile([P, S], F32, name="raw_0", offset=2048, align_bytes=64)
         early = raw_0[:, 0 : 2 * PASS]
         other = raw_0[:, 2 * PASS :]
@@ -115,6 +112,10 @@ def tile_moe_bdw_lin_none_kernel(tc, xT, dyT, gate, offs, out):
         nc.vector.tensor_copy(other[:, 0:512], look_up(dy_all[0], 1024, 1536))
         nc.scalar.activation(early[:, 512:1024], look_up(dy_all[0], 512, 1024), COPY)
         nc.scalar.activation(other[:, 512:1024], look_up(dy_all[0], 1536, S), COPY)
+        for q in range(2):
+            nc.vector.tensor_copy(gates[:, q, :], backs[q][:, :, 0])
+        nc.vector.tensor_copy(early1[:, 510:514], gates[:, 1, :])
+        nc.vector.tensor_copy(last_gates, gates[:, 1, :].rearrange("p (a b) -> p a b", a=2))
         rounded = [sbuf([P, PASS], BF16, f"rounded0{j}") for j in range(2)]
         for j in range(2):
             nc.gpsimd.tensor_tensor(rounded[j][:], other[:, j * PASS : (j + 1) * PASS], gate_row[:, j * PASS : (j + 1) * PASS], MULT)

@@ -171,8 +171,10 @@ def tile_moe_bdw_lin_none_kernel(tc, xT, dyT, gate, offs, out):
             turn_words(pair[:, j, :, :], j)
         rows = sbuf([P, 2 * PASS], BF16, "rows_x01")
         pairs_out(nc.vector.tensor_copy, rows[:], pair)
-        quantize_g(2, 6, rows_mid[:])
+        quantize_g(4, 6, rows_mid[:, 2 * PASS :])
         quantize(codes_x[:, 0 : 2 * K], scales_x[:, 0 : 2 * K], rows[:])
+        codes_mid = sbuf([P, 2 * P], U32, "codes_mid", tag="rows_x01")[:]
+        quantize(codes_mid, scales_g[:, 2 * P : 4 * P], rows_mid[:, 0 : 2 * PASS])
         quantize_g(6, 8, rows_w1[:])
         for q, b in ((3, 1), (2, 3)):
             single = bank(b, [P, 2, P])
@@ -182,6 +184,7 @@ def tile_moe_bdw_lin_none_kernel(tc, xT, dyT, gate, offs, out):
             quantize(codes_x[:, q * K : (q + 1) * K], scales_x[:, q * K : (q + 1) * K], rows[:])
 
         words_g = [codes_g[:, i * P : (i + 1) * P] for i in range(2 * PASSES)]
+        words_g[2:4] = [codes_mid[:, 0:P], codes_mid[:, P:]]
         accs = {(0, 0): bank(2, [P, P]), (0, 1): bank(0, [P, P]), (1, 0): bank(6, [P, P]), (1, 1): bank(7, [P, P])}
         for q, h in ((0, 0), (1, 0), (0, 1), (1, 1), (3, 0), (3, 1), (2, 0), (2, 1)):
             e = q // 2

@@ -35,7 +35,7 @@ def tile_moe_bdw_lin_none_kernel(tc, xT, dyT, gate, offs, out):
             return held.tile(shape, dtype, name=name, tag=tag or name, align_bytes=64)
 
         offsets = held.tile([P, S // 16], U16, name="offsets")
-        gates = sbuf([P, 2, 4], F32, "gates")
+        gates = sbuf([P, PASSES, 4], F32, "gates")
         dy_all = [held.tile([P, T], F32, name=f"dy_all{h}") for h in range(2)]
         x_all = held.tile([P, T], F32, name="x_all")
         gate_runs = held.tile([P, 16], F32, name="gate_runs")
@@ -58,9 +58,9 @@ def tile_moe_bdw_lin_none_kernel(tc, xT, dyT, gate, offs, out):
                 nc.scalar.activation(places, spread[:].rearrange("p r k -> p k r"), COPY)
             else:
                 nc.vector.tensor_copy(places, spread[:].rearrange("p r k -> p k r"))
-        backs = [bank(2 + q, [P, 4, P]) for q in range(2)]
+        backs = [bank(2 + q, [P, 4, P]) for q in range(PASSES)]
         for t in range(4):
-            for q in range(2):
+            for q in range(PASSES):
                 nc.tensor.transpose(backs[q][:, t, :], by_place[:, t, q * P : (q + 1) * P], identity[:])
         gate_row = held.tile([P, 2 * PASS], F32, name="gate_row")
         nc.vector.tensor_copy(gate_row[:].rearrange("p (s t) -> p s t", t=4), by_place[:, :, 2 * P :].rearrange("p t s -> p s t"))
@@ -105,28 +105,22 @@ def tile_moe_bdw_lin_none_kernel(tc, xT, dyT, gate, offs, out):
         even_x = sbuf([P, 1568], BF16, "even_x")[:]
         last_gates = even_x.bitcast(F32)[:, 250:770].rearrange("p (a b c) -> p a b c", a=2, b=2)[:, :, :, 0]
         raw_0 = lap.tile([P, S], F32, name="raw_0", offset=2048, align_bytes=64)
-        early = raw_0[:, 0 : 2 * PASS]
-        other = raw_0[:, 2 * PASS :]
-        nc.vector.tensor_copy(early[:, 0:256], look_up(dy_all[0], 0, 256))
-        nc.scalar.activation(early[:, 256:512], look_up(dy_all[0], 256, 512), COPY)
-        nc.vector.tensor_copy(other[:, 0:512], look_up(dy_all[0], 1024, 1536))
-        nc.scalar.activation(early[:, 512:1024], look_up(dy_all[0], 512, 1024), COPY)
-        nc.scalar.activation(other[:, 512:1024], look_up(dy_all[0], 1536, S), COPY)
-        for q in range(2):
+        nc.vector.tensor_copy(raw_0[:, 0:256], look_up(dy_all[0], 0, 256))
+        nc.scalar.activation(raw_0[:, 256:512], look_up(dy_all[0], 256, 512), COPY)
+        nc.vector.tensor_copy(raw_0[:, 1024:1280], look_up(dy_all[0], 1024, 1280))
+        nc.scalar.activation(raw_0[:, 512:1024], look_up(dy_all[0], 512, 1024), COPY)
+        nc.scalar.activation(raw_0[:, 1280:1536], look_up(dy_all[0], 1280, 1536), COPY)
+        nc.scalar.activation(raw_0[:, 1536:S], look_up(dy_all[0], 1536, S), COPY)
+        for q in range(PASSES):
             nc.vector.tensor_copy(gates[:, q, :], backs[q][:, :, 0])
         nc.vector.tensor_copy(early1[:, 510:514], gates[:, 1, :])
         nc.vector.tensor_copy(last_gates, gates[:, 1, :].rearrange("p (a b) -> p a b", a=2))
-        rounded = [sbuf([P, PASS], BF16, f"rounded0{j}") for j in range(2)]
-        for j in range(2):
-            nc.gpsimd.tensor_tensor(rounded[j][:], other[:, j * PASS : (j + 1) * PASS], gate_row[:, j * PASS : (j + 1) * PASS], MULT)
-        turned = [turn_values(early, q, q) for q in range(2)]
-        rows_b0 = sbuf([P, 2 * PASS], BF16, "rows_b0")
-        rows_mid = sbuf([P, 4 * PASS], BF16, "rows_mid")
-        gate_and_round(rows_b0[:, 0:PASS], gates[:, 0:1, :], turned[0])
-        gate_and_round(rows_b0[:, PASS:], early1[:, 510:514].unsqueeze(1), turned[1])
-        pairs = bank(0, [P, 2, 2, P])
-        for j in range(2):
-            turn_pairs(pairs[:, j, :, :], rounded[j][:])
+        waiting = [turn_values(raw_0, q, q) for q in range(PASSES)]
+        for q, gate_words in enumerate((gates[:, 0:1, :], early1[:, 510:514].unsqueeze(1))):
+            rows = sbuf([P, PASS], BF16, f"rows_g0{q}")
+            gate_and_round(rows[:], gate_words, waiting[q])
+            quantize_g(q, q + 1, rows[:])
+        rows_mid = sbuf([P, 4 * PASS], BF16, "rows_mid", tag="rows_g01")
 
         other = lap.tile([P, 2 * PASS], F32, name="other1", offset=10240, align_bytes=64)
         nc.scalar.activation(early1[:, 0:256], look_up(dy_all[1], 0, 256), COPY)
@@ -134,8 +128,8 @@ def tile_moe_bdw_lin_none_kernel(tc, xT, dyT, gate, offs, out):
         nc.vector.tensor_copy(early1[:, 512:1024], look_up(dy_all[1], 512, 1024))
         for j in range(2):
             nc.scalar.activation(other[:, j * PASS : (j + 1) * PASS], look_up(dy_all[1], (2 + j) * PASS, (3 + j) * PASS), COPY)
-        quantize_g(0, 2, rows_b0[:])
-        pairs_out(nc.scalar.copy, rows_mid[:, 0 : 2 * PASS], pairs)
+        for q in (2, 3):
+            gate_and_round(rows_mid[:, (q - 2) * PASS : (q - 1) * PASS], gates[:, q : q + 1, :], waiting[q])
         turned = [turn_values(early1, q, 4 + q) for q in range(2)]
         gate_and_round(rows_mid[:, 2 * PASS : 3 * PASS], gates[:, 0:1, :], turned[0])
         rows_w1 = sbuf([P, 2 * PASS], BF16, "rows_w1")

from contextlib import ExitStack

import concourse.mybir as mybir
from concourse.masks import make_identity

K, T, E, C, N = 128, 4096, 2, 1024, 256
S = E * C
P = 128
PASS = 512
PASSES = S // PASS
FLOPS = 2 * S * K * N

F32 = mybir.dt.float32
BF16 = mybir.dt.bfloat16
U32 = mybir.dt.uint32
U16 = mybir.dt.uint16
U8 = mybir.dt.uint8
FP8X4 = mybir.dt.float8_e4m3fn_x4
MULT = mybir.AluOpType.mult
ADD = mybir.AluOpType.add
COPY = mybir.ActivationFunctionType.Copy


def tile_moe_bdw_lin_none_kernel(tc, xT, dyT, gate, offs, out):
    nc = tc.nc
    with ExitStack() as ctx:
        held = ctx.enter_context(tc.tile_pool(name="held", bufs=1))
        lap = ctx.enter_context(tc.tile_pool(name="lap", bufs=1))
        psum = ctx.enter_context(tc.psum_pool(name="psum", bufs=1))

        def bank(b, shape):
            return psum.tile(shape, F32, name=f"bank{b}", tag=f"bank{b}")

        def sbuf(shape, dtype, name, tag=None):
            return held.tile(shape, dtype, name=name, tag=tag or name, align_bytes=64)

        offsets = held.tile([P, S // 16], U16, name="offsets")
        gates = sbuf([P, PASSES, 4], F32, "gates")
        dy_all = [held.tile([P, T], F32, name=f"dy_all{h}") for h in range(2)]
        x_all = held.tile([P, T], F32, name="x_all")
        gate_runs = held.tile([P, 16], F32, name="gate_runs")
        nc.sync.dma_start(gate_runs[:], gate[0:1, :].rearrange("o (k j) -> k (o j)", j=16))
        nc.sync.dma_start(offsets[:], offs)
        for h in range(2):
            nc.scalar.dma_start(dy_all[h][:], dyT[h * P : (h + 1) * P, :])
        nc.scalar.dma_start(x_all[:], xT)

        identity = held.tile([P, P], F32, name="identity")
        make_identity(nc, identity[:])

        by_place = lap.tile([P, 4, PASS], F32, name="by_place", offset=8192, align_bytes=64)
        for t in range(4):
            spread = bank(4 + t, [P, 4, P])
            for r in range(4):
                nc.tensor.transpose(spread[:, r, :], gate_runs[:, 4 * r + t : 4 * r + t + 1].to_broadcast([P, P]), identity[:])
            places = by_place[:, t, :].rearrange("p (k r) -> p k r", r=4)
            if t % 2 == 0:
                nc.scalar.activation(places, spread[:].rearrange("p r k -> p k r"), COPY)
            else:
                nc.vector.tensor_copy(places, spread[:].rearrange("p r k -> p k r"))
        backs = [bank(2 + q, [P, 4, P]) for q in range(PASSES)]
        for t in range(4):
            for q in range(PASSES):
                nc.tensor.transpose(backs[q][:, t, :], by_place[:, t, q * P : (q + 1) * P], identity[:])
        gate_row = held.tile([P, 2 * PASS], F32, name="gate_row")
        nc.vector.tensor_copy(gate_row[:].rearrange("p (s t) -> p s t", t=4), by_place[:, :, 2 * P :].rearrange("p t s -> p s t"))

        codes_g = sbuf([P, 2 * PASSES * P], U32, "codes_g")
        scales_g = sbuf([P, 2 * PASSES * P], U8, "scales_g")

        def look_up(window, a, b):
            return window[:].indirect(offsets[:, a // 16 : b // 16])

        def quantize(codes, scales, rows):
            nc.vector.quantize_mx(out=codes.bitcast(FP8X4), scales=scales, in_=rows)

        def quantize_g(a, b, rows):
            quantize(codes_g[:, a * P : b * P], scales_g[:, a * P : b * P], rows)

        def turn_values(picked, q, b):
            turned = bank(b, [P, 4, P])
            for t in range(4):
                nc.tensor.transpose(turned[:, t, :], picked[:, q * PASS + t : (q + 1) * PASS : 4], identity[:])
            return turned

        def gate_and_round(rows, gate_words, turned):
            nc.vector.tensor_tensor(
                rows.rearrange("p (n t) -> p n t", t=4),
                turned[:].rearrange("p t n -> p n t"),
                gate_words.to_broadcast([P, P, 4]),
                MULT,
            )

        def pairs_out(copy, rows, pair):
            copy(out=rows.bitcast(F32).rearrange("p (q k u) -> p q k u", q=2, u=2), in_=pair[:].rearrange("p q u k -> p q k u"))

        def words_out(copy, rows, single):
            copy(out=rows.bitcast(F32).rearrange("p (k u) -> p k u", u=2), in_=single[:].rearrange("p u k -> p k u"))

        def turn_pairs(turned, rounded):
            for u in range(2):
                nc.tensor.transpose(turned[:, u, :], rounded.bitcast(F32)[:, u:256:2], identity[:])

        early1 = lap.tile([P, 2 * PASS], F32, name="early1", offset=14336, align_bytes=64)
        even_x = sbuf([P, 1568], BF16, "even_x")[:]
        last_gates = even_x.bitcast(F32)[:, 250:770].rearrange("p (a b c) -> p a b c", a=2, b=2)[:, :, :, 0]
        raw_0 = lap.tile([P, S], F32, name="raw_0", offset=2048, align_bytes=64)
        nc.vector.tensor_copy(raw_0[:, 0:256], look_up(dy_all[0], 0, 256))
        nc.scalar.activation(raw_0[:, 256:512], look_up(dy_all[0], 256, 512), COPY)
        nc.vector.tensor_copy(raw_0[:, 1024:1280], look_up(dy_all[0], 1024, 1280))
        nc.scalar.activation(raw_0[:, 512:1024], look_up(dy_all[0], 512, 1024), COPY)
        nc.scalar.activation(raw_0[:, 1280:1536], look_up(dy_all[0], 1280, 1536), COPY)
        nc.scalar.activation(raw_0[:, 1536:S], look_up(dy_all[0], 1536, S), COPY)
        for q in range(PASSES):
            nc.vector.tensor_copy(gates[:, q, :], backs[q][:, :, 0])
        nc.vector.tensor_copy(early1[:, 510:514], gates[:, 1, :])
        nc.vector.tensor_copy(last_gates, gates[:, 1, :].rearrange("p (a b) -> p a b", a=2))
        waiting = [turn_values(raw_0, q, q) for q in range(PASSES)]
        for q, gate_words in enumerate((gates[:, 0:1, :], early1[:, 510:514].unsqueeze(1))):
            rows = sbuf([P, PASS], BF16, f"rows_g0{q}")
            gate_and_round(rows[:], gate_words, waiting[q])
            quantize_g(q, q + 1, rows[:])
        rows_mid = sbuf([P, 4 * PASS], BF16, "rows_mid", tag="rows_g01")

        other = lap.tile([P, 2 * PASS], F32, name="other1", offset=10240, align_bytes=64)
        nc.scalar.activation(early1[:, 0:256], look_up(dy_all[1], 0, 256), COPY)
        nc.vector.tensor_copy(early1[:, 256:512], look_up(dy_all[1], 256, 512))
        nc.vector.tensor_copy(early1[:, 512:1024], look_up(dy_all[1], 512, 1024))
        for j in range(2):
            nc.scalar.activation(other[:, j * PASS : (j + 1) * PASS], look_up(dy_all[1], (2 + j) * PASS, (3 + j) * PASS), COPY)
        for q in (2, 3):
            gate_and_round(rows_mid[:, (q - 2) * PASS : (q - 1) * PASS], gates[:, q : q + 1, :], waiting[q])
        turned = [turn_values(early1, q, 4 + q) for q in range(2)]
        gate_and_round(rows_mid[:, 2 * PASS : 3 * PASS], gates[:, 0:1, :], turned[0])
        rows_w1 = sbuf([P, 2 * PASS], BF16, "rows_w1")
        rounded = [sbuf([P, PASS], BF16, f"rounded1{j}") for j in range(2)]
        for j in range(2):
            nc.gpsimd.tensor_tensor(rounded[j][:], other[:, j * PASS : (j + 1) * PASS], gate_row[:, j * PASS : (j + 1) * PASS], MULT)
        nc.vector.tensor_tensor(
            rows_mid[:, 3 * PASS :].rearrange("p (n a b) -> p n a b", a=2, b=2),
            turned[1][:].rearrange("p (a b) n -> p n a b", a=2),
            last_gates.unsqueeze(1).to_broadcast([P, P, 2, 2]),
            MULT,
        )
        singles = [bank(4 + j, [P, 2, P]) for j in range(2)]
        for j in range(2):
            turn_pairs(singles[j], rounded[j][:])
        words_out(nc.vector.tensor_copy, rows_w1[:, 0:PASS], singles[0])

        odd_x = lap.tile([P, PASS], BF16, name="odd_x", offset=16384, align_bytes=64)[:]
        nc.vector.tensor_copy(even_x[:, 0:512], look_up(x_all, 0, 512))
        nc.scalar.activation(odd_x[:, 0:512], look_up(x_all, 512, 1024), COPY)
        nc.scalar.activation(even_x[:, 1024:1536], look_up(x_all, 1536, S), COPY)
        nc.vector.tensor_copy(even_x[:, 512:896], look_up(x_all, 1024, 1408))
        nc.scalar.activation(even_x[:, 896:1024], look_up(x_all, 1408, 1536), COPY)
        words_out(nc.scalar.copy, rows_w1[:, PASS:], singles[1])

        def turn_words(turned, q):
            turn_pairs(turned, (even_x[:, 0:PASS], odd_x, even_x[:, PASS : 2 * PASS], even_x[:, 2 * PASS : 3 * PASS])[q])

        codes_x = sbuf([P, PASSES * K], U32, "codes_x")
        scales_x = sbuf([P, PASSES * K], U8, "scales_x")
        pair = bank(2, [P, 2, 2, P])
        for j in (1, 0):
            turn_words(pair[:, j, :, :], j)
        rows = sbuf([P, 2 * PASS], BF16, "rows_x01")
        pairs_out(nc.vector.tensor_copy, rows[:], pair)
        quantize_g(4, 6, rows_mid[:, 2 * PASS :])
        quantize(codes_x[:, 0 : 2 * K], scales_x[:, 0 : 2 * K], rows[:])
        codes_mid = sbuf([P, 2 * P], U32, "codes_mid", tag="rows_x01")[:]
        quantize(codes_mid, scales_g[:, 2 * P : 4 * P], rows_mid[:, 0 : 2 * PASS])
        quantize_g(6, 8, rows_w1[:])
        for q, b in ((3, 1), (2, 3)):
            single = bank(b, [P, 2, P])
            turn_words(single, q)
            rows = sbuf([P, PASS], BF16, f"rows_x{q}")
            words_out(nc.scalar.copy, rows[:], single)
            quantize(codes_x[:, q * K : (q + 1) * K], scales_x[:, q * K : (q + 1) * K], rows[:])

        words_g = [codes_g[:, i * P : (i + 1) * P] for i in range(2 * PASSES)]
        words_g[2:4] = [codes_mid[:, 0:P], codes_mid[:, P:]]
        accs = {(0, 0): bank(2, [P, P]), (0, 1): bank(0, [P, P]), (1, 0): bank(6, [P, P]), (1, 1): bank(7, [P, P])}
        for q, h in ((0, 0), (1, 0), (0, 1), (1, 1), (3, 0), (3, 1), (2, 0), (2, 1)):
            e = q // 2
            closes = q in (1, 2)
            nc.tensor.matmul_mx(
                out=accs[e, h][:],
                lhsT=codes_x[:, q * K : (q + 1) * K].bitcast(FP8X4),
                lhsT_scale=scales_x[:, q * K : (q + 1) * K],
                rhs=words_g[4 * h + q].bitcast(FP8X4),
                rhs_scale=scales_g[:, (4 * h + q) * P : (4 * h + q + 1) * P],
                start=not closes,
                stop=closes,
            )
            if closes:
                res = held.tile([P, P], F32, name=f"res{e}{h}")
                if (e, h) == (1, 1):
                    nc.vector.tensor_copy(res[:], accs[e, h][:])
                else:
                    nc.scalar.copy(out=res[:], in_=accs[e, h][:])
                nc.sync.dma_start(out[e, :, h * P : (h + 1) * P], res[:])
